import numpy as np
import ml_dtypes


def mxq(x, axis, fmt="e4m3"):
    dtype, down = {"e4m3": (ml_dtypes.float8_e4m3fn, 7), "e5m2": (ml_dtypes.float8_e5m2, 14)}[fmt]
    v = np.moveaxis(np.asarray(x, np.float32).astype(ml_dtypes.bfloat16).astype(np.float64), axis, -1)
    blocks = v.reshape(v.shape[:-1] + (-1, 32))
    amax = np.abs(blocks).max(-1, keepdims=True)
    byte = np.maximum(np.where(amax > 0, np.frexp(amax)[1] - 1 + 127, 0) - down, 1)
    scale = np.exp2(byte - 127.0)
    codes = (blocks / scale).astype(np.float32).astype(dtype).astype(np.float64)
    return np.moveaxis((codes * scale).reshape(v.shape), -1, axis)


WIDE = False


def mx_kscale(k):
    if not WIDE:
        return np.ones(k)
    levels = np.array([10, -10, 5, -5, 0])
    if k % 512:
        return np.exp2(np.random.permutation(np.resize(levels, k // 32))).repeat(32)
    a = np.empty((k // 512, 16))
    for p in range(k // 512):
        a[p, :8] = np.random.permutation(np.resize(levels, 8))
        for g in range(8):
            far = levels[np.abs(levels - a[p, g]) >= 10]
            a[p, g + 8] = far[np.random.randint(len(far))]
    return np.exp2(a.ravel()).repeat(32)


def f64(x):
    return np.asarray(x).astype(np.float64)


def striped(idx):
    return np.tile(idx.reshape(-1, 16).T, (8, 1)).astype(np.uint16)


def unstriped(offs):
    return offs[:16].T.reshape(-1).astype(np.int64)


E2M1 = np.array([0.0, 0.5, 1.0, 1.5, 2.0, 3.0, 4.0, 6.0, -0.0, -0.5, -1.0, -1.5, -2.0, -3.0, -4.0, -6.0])


def pack_weight(w, fmt):
    k, n = w.shape
    w = f64(np.asarray(w, np.float32).astype(ml_dtypes.bfloat16)).reshape(k // 32, 32, n)
    amax = np.abs(w).max(1)
    if fmt == "e4m3":
        byte = np.frexp(amax)[1] - 1 + 127 - 7
    else:
        mant, ex = np.frexp(amax / 6.0)
        byte = np.where(mant > 0.5, ex, ex - 1) + 127
    byte = np.clip(np.where(amax > 0, byte, 1), 1, 254)
    scaled = (w * np.exp2(127.0 - byte)[:, None, :]).reshape(k, n).astype(np.float32)
    by_word = np.ascontiguousarray(scaled.reshape(k // 512, 128, 4, n).transpose(0, 1, 3, 2))
    if fmt == "e4m3":
        words = by_word.astype(ml_dtypes.float8_e4m3fn).view(np.uint8)
    else:
        c = by_word.astype(ml_dtypes.float4_e2m1fn).view(np.uint8) & 0xF
        words = (c[..., 0::2] | (c[..., 1::2] << 4)).reshape(k // 512, 128, 2 * n)
    return np.ascontiguousarray(words), np.ascontiguousarray(byte.astype(np.uint8).reshape(k // 512, 16, n))


def unpack_weight(words, scales, fmt):
    g, _, n = scales.shape
    words = np.ascontiguousarray(words).reshape(g, 128, n, -1)
    if fmt == "e4m3":
        vals = words.view(ml_dtypes.float8_e4m3fn).astype(np.float64)
    else:
        nib = np.empty((g, 128, n, 4), np.uint8)
        nib[..., 0::2] = words & 0xF
        nib[..., 1::2] = words >> 4
        vals = E2M1[nib]
    vals = vals * np.repeat(np.exp2(scales.astype(np.float64) - 127.0), 8, axis=1)[..., None]
    return vals.transpose(0, 1, 3, 2).reshape(g * 512, n)


K, M, T, S = 512, 512, 2048, 1024


def setup_inputs():
    n = np.random.standard_normal
    s = mx_kscale(K)[:, None]
    s2 = mx_kscale(512)[:, None]
    v = pack_weight(n((K, T)) * s, "e4m3")
    p_w4 = pack_weight(n((K, M)) / np.sqrt(K) / s, "e2m1")
    return {
        "tab_words": v[0],
        "tab_scales": v[1],
        "w4_words": p_w4[0],
        "w4_scales": p_w4[1],
        "c": (n((512, S)) * s2).astype(np.float32),
        "u": (n((512, M)) / np.sqrt(512) / s2).astype(np.float32),
        "rT": n((M, T)).astype(np.float32),
        "offs": striped(np.random.permutation(T)[:S]),
    }


def reference(tab_words, tab_scales, w4_words, w4_scales, c, u, rT, offs):
    tab_ = unpack_weight(tab_words, tab_scales, "e4m3")[:, unstriped(offs)]
    w4_ = unpack_weight(w4_words, w4_scales, "e2m1")
    c_ = mxq(f64(c), 0, "e4m3")
    u_ = mxq(f64(u), 0, "e4m3")
    y = w4_.T @ tab_ + u_.T @ c_
    return (y) + f64(rT)[:, unstriped(offs)]

@@ -1,0 +1,181 @@
+from contextlib import ExitStack
+
+import concourse.mybir as mybir
+
+K, M, T, S = 512, 512, 2048, 1024
+FLOPS = 2 * 2 * K * M * S
+
+F32 = mybir.dt.float32
+BF16 = mybir.dt.bfloat16
+I32 = mybir.dt.int32
+U32 = mybir.dt.uint32
+U16 = mybir.dt.uint16
+U8 = mybir.dt.uint8
+FP8X4 = mybir.dt.float8_e4m3fn_x4
+FP4X4 = mybir.dt.float4_e2m1fn_x4
+ADD = mybir.AluOpType.add
+
+P = 128
+PACK = 4
+BLOCKS = M // P
+CHUNK = 256
+CHUNKS = S // CHUNK
+PAIR = 2
+N_FP4 = 128
+STRIPE = 16
+
+
+def tile_list_tabres_none_kernel(
+    tc, tab_words, tab_scales, w4_words, w4_scales, c, u, rT, offs, out
+):
+    nc = tc.nc
+    with ExitStack() as ctx:
+        keep = ctx.enter_context(tc.tile_pool(name="keep", bufs=1))
+        psum = ctx.enter_context(tc.psum_pool(name="psum", bufs=1))
+
+        offsets = keep.tile([P, S // STRIPE], U16, name="offsets")
+        tab_w = keep.tile([P, T], U32, name="tab_w", align_bytes=64)
+        tab_s = keep.tile([P, T], U8, name="tab_s", align_bytes=64)
+        tab_rows = keep.tile([P, T], U8, name="tab_rows", align_bytes=64)
+        w4_w = keep.tile([P, 2 * M], U8, name="w4_w", align_bytes=64)
+        w4_s = keep.tile([P, M], U8, name="w4_s", align_bytes=64)
+        u_raw = keep.tile([P, PACK, M], F32, name="u_raw", align_bytes=64)
+        u_bf = [keep.tile([P, CHUNK, PACK], BF16, name="u_bf%d" % h, align_bytes=64) for h in range(M // CHUNK)]
+        u_w = keep.tile([P, M], U32, name="u_w", align_bytes=64)
+        u_s = keep.tile([P, M], U8, name="u_s", align_bytes=64)
+        pick_w = keep.tile([P, S], U32, name="pick_w", align_bytes=64)
+        pick_s = keep.tile([P, S], U8, name="pick_s", align_bytes=64)
+        res = [keep.tile([P, T], F32, name="res%d" % b, align_bytes=64) for b in range(BLOCKS)]
+        pick_r = keep.tile([P, BLOCKS, S], F32, name="pick_r", align_bytes=64)
+        c_raw = [keep.tile([P, PACK, CHUNK], F32, name="c_raw%d" % q, align_bytes=64) for q in range(CHUNKS)]
+        c_bf = [keep.tile([P, CHUNK, PACK], BF16, name="c_bf%d" % q, align_bytes=64) for q in range(CHUNKS)]
+        c_w = [keep.tile([P, CHUNK], U32, name="c_w%d" % q, align_bytes=64) for q in range(CHUNKS)]
+        c_s = [keep.tile([P, CHUNK], U8, name="c_s%d" % q, align_bytes=64) for q in range(CHUNKS)]
+        banks = {}
+        staged = {}
+        for q in range(CHUNKS):
+            for h in range(BLOCKS // PAIR):
+                banks[q, h] = psum.tile([P, PAIR, CHUNK], F32, name="bank%d_%d" % (q, h))
+                staged[q, h] = keep.tile([P, PAIR, CHUNK], F32, name="staged%d_%d" % (q, h), align_bytes=64)
+
+        c_rows = c.rearrange("(p t) j -> p t j", t=PACK)
+        out_rows = out.rearrange("(b p) j -> p b j", p=P)
+
+        def load_scales(plane, rows):
+            for r in range(4):
+                nc.sync.dma_start(out=plane[r:P:32, :].bitcast(I32), in_=rows[r:16:4, :].bitcast(I32))
+
+        def load_scales_by_quadrant(plane, rows):
+            for quad in range(4):
+                nc.sync.dma_start(
+                    out=plane[32 * quad : 32 * quad + 4, :].bitcast(I32), in_=rows[4 * quad : 4 * quad + 4, :].bitcast(I32)
+                )
+
+        def load_res(b):
+            nc.sync.dma_start(out=res[b][:], in_=rT[b * P : (b + 1) * P, :])
+
+        def load_c(q):
+            nc.sync.dma_start(out=c_raw[q][:], in_=c_rows[:, :, q * CHUNK : (q + 1) * CHUNK])
+
+        def interleave(dst, raw):
+            nc.scalar.copy(
+                out=dst[:].rearrange("p (g i) t -> p g t i", i=4),
+                in_=raw.rearrange("p t (g i) -> p g t i", i=4),
+            )
+
+        def quantize(words, scales, grouped):
+            nc.vector.quantize_mx(
+                out=words.bitcast(FP8X4), scales=scales, in_=grouped[:].rearrange("p w t -> p (w t)")
+            )
+
+        def gather_res(b, j0, j1):
+            nc.vector.tensor_copy(
+                out=pick_r[:, b, j0:j1], in_=res[b][:].indirect(offsets[:, j0 // STRIPE : j1 // STRIPE])
+            )
+
+        def table_passes(q, h):
+            first = True
+            for e in range(PAIR):
+                b = PAIR * h + e
+                for j0 in range(0, CHUNK, N_FP4):
+                    cols = slice(q * CHUNK + j0, q * CHUNK + j0 + N_FP4)
+                    nc.tensor.matmul_mx(
+                        out=banks[q, h][:, e, j0 : j0 + N_FP4],
+                        lhsT=w4_w[:, 2 * b * P : 2 * (b + 1) * P].bitcast(FP4X4),
+                        lhsT_scale=w4_s[:, b * P : (b + 1) * P],
+                        rhs=pick_w[:, cols].bitcast(FP8X4),
+                        rhs_scale=pick_s[:, cols],
+                        start=first,
+                        stop=False,
+                    )
+                    first = False
+
+        def feature_passes(q, h):
+            for e in range(PAIR):
+                b = PAIR * h + e
+                nc.tensor.matmul_mx(
+                    out=banks[q, h][:, e, :],
+                    lhsT=u_w[:, b * P : (b + 1) * P].bitcast(FP8X4),
+                    lhsT_scale=u_s[:, b * P : (b + 1) * P],
+                    rhs=c_w[q][:].bitcast(FP8X4),
+                    rhs_scale=c_s[q][:],
+                    start=False,
+                    stop=(e == PAIR - 1),
+                )
+
+        def finish(q, h):
+            cols = slice(q * CHUNK, (q + 1) * CHUNK)
+            blocks = slice(PAIR * h, PAIR * (h + 1))
+            nc.vector.tensor_tensor(out=staged[q, h][:], in0=banks[q, h][:], in1=pick_r[:, blocks, cols], op=ADD)
+            nc.sync.dma_start(out=out_rows[:, blocks, cols], in_=staged[q, h][:])
+
+        def prepare_c(q):
+            interleave(c_bf[q], c_raw[q][:])
+            quantize(c_w[q][:], c_s[q][:], c_bf[q])
+            for h in range(BLOCKS // PAIR):
+                feature_passes(q, h)
+
+        nc.vector.memset(tab_s[:].bitcast(I32), 0)
+
+        nc.sync.dma_start(offsets[:], offs)
+        load_scales_by_quadrant(tab_rows, tab_scales[0])
+        nc.sync.dma_start(out=tab_w[:].bitcast(I32), in_=tab_words[0].rearrange("p t i -> p (t i)").bitcast(I32))
+        nc.sync.dma_start(out=u_raw[:], in_=u.rearrange("(p t) n -> p t n", t=PACK))
+        load_res(0)
+        nc.sync.dma_start(out=w4_w[:].bitcast(I32), in_=w4_words[0].bitcast(I32))
+        load_scales(w4_s, w4_scales[0])
+        load_res(1)
+        load_res(2)
+        load_c(0)
+        load_res(3)
+        for q in range(1, CHUNKS):
+            load_c(q)
+
+        for quad in range(0, P, 32):
+            live = slice(quad, quad + 4)
+            nc.vector.tensor_copy(out=tab_s[live, :].bitcast(I32), in_=tab_rows[live, :].bitcast(I32))
+        nc.vector.tensor_copy(out=pick_s[:], in_=tab_s[:].indirect(offsets[:]))
+        nc.vector.tensor_copy(out=pick_w[:], in_=tab_w[:].indirect(offsets[:]))
+        for h in range(M // CHUNK):
+            cols = slice(h * CHUNK, (h + 1) * CHUNK)
+            interleave(u_bf[h], u_raw[:, :, cols])
+            quantize(u_w[:, cols], u_s[:, cols], u_bf[h])
+        for q in range(CHUNKS):
+            for h in range(BLOCKS // PAIR):
+                table_passes(q, h)
+        for b in range(BLOCKS - 1):
+            gather_res(b, 0, S)
+        last = BLOCKS - 1
+        prepare_c(0)
+        finish(0, 0)
+        gather_res(last, 0, CHUNK)
+        gather_res(last, CHUNK, 2 * CHUNK)
+        finish(0, 1)
+        gather_res(last, 2 * CHUNK, 3 * CHUNK)
+        prepare_c(1)
+        gather_res(last, 3 * CHUNK, S)
+        for q in range(1, CHUNKS):
+            if q + 1 < CHUNKS:
+                prepare_c(q + 1)
+            finish(q, 0)
+            finish(q, 1)

@@ -18,11 +18,11 @@ ADD = mybir.AluOpType.add
 P = 128
 PACK = 4
 BLOCKS = M // P
-CHUNK = 256
-CHUNKS = S // CHUNK
-PAIR = 2
+BANK = 512
 N_FP4 = 128
 STRIPE = 16
+CHUNKS = ((0, 512), (512, 1024))
+C_LOADS = CHUNKS
 
 
 def tile_list_tabres_none_kernel(
@@ -33,59 +33,70 @@ def tile_list_tabres_none_kernel(
         keep = ctx.enter_context(tc.tile_pool(name="keep", bufs=1))
         psum = ctx.enter_context(tc.psum_pool(name="psum", bufs=1))
 
+        def sbuf(name, shape, dtype):
+            return keep.tile(shape, dtype, name=name, align_bytes=64)
+
         offsets = keep.tile([P, S // STRIPE], U16, name="offsets")
-        tab_w = keep.tile([P, T], U32, name="tab_w", align_bytes=64)
-        tab_s = keep.tile([P, T], U8, name="tab_s", align_bytes=64)
-        tab_rows = keep.tile([P, T], U8, name="tab_rows", align_bytes=64)
-        w4_w = keep.tile([P, 2 * M], U8, name="w4_w", align_bytes=64)
-        w4_s = keep.tile([P, M], U8, name="w4_s", align_bytes=64)
-        u_raw = keep.tile([P, PACK, M], F32, name="u_raw", align_bytes=64)
-        u_bf = [keep.tile([P, CHUNK, PACK], BF16, name="u_bf%d" % h, align_bytes=64) for h in range(M // CHUNK)]
-        u_w = keep.tile([P, M], U32, name="u_w", align_bytes=64)
-        u_s = keep.tile([P, M], U8, name="u_s", align_bytes=64)
-        pick_w = keep.tile([P, S], U32, name="pick_w", align_bytes=64)
-        pick_s = keep.tile([P, S], U8, name="pick_s", align_bytes=64)
-        res = [keep.tile([P, T], F32, name="res%d" % b, align_bytes=64) for b in range(BLOCKS)]
-        pick_r = keep.tile([P, BLOCKS, S], F32, name="pick_r", align_bytes=64)
-        c_raw = [keep.tile([P, PACK, CHUNK], F32, name="c_raw%d" % q, align_bytes=64) for q in range(CHUNKS)]
-        c_bf = [keep.tile([P, CHUNK, PACK], BF16, name="c_bf%d" % q, align_bytes=64) for q in range(CHUNKS)]
-        c_w = [keep.tile([P, CHUNK], U32, name="c_w%d" % q, align_bytes=64) for q in range(CHUNKS)]
-        c_s = [keep.tile([P, CHUNK], U8, name="c_s%d" % q, align_bytes=64) for q in range(CHUNKS)]
+        tab_w = sbuf("tab_w", [P, T], U32)
+        tab_s = sbuf("tab_s", [P, T], U8)
+        w4_w = sbuf("w4_w", [P, 2 * M], U8)
+        w4_s = sbuf("w4_s", [P, M], U8)
+        u_raw = sbuf("u_raw", [P, PACK, M], F32)
+        u_bf = sbuf("u_bf", [P, M, PACK], BF16)
+        u_w = sbuf("u_w", [P, M], U32)
+        u_s = sbuf("u_s", [P, M], U8)
+        pick_w = sbuf("pick_w", [P, S], U32)
+        pick_s = sbuf("pick_s", [P, S], U8)
+        res = [sbuf("res%d" % b, [P, T], F32) for b in range(BLOCKS)]
+        pick_r = sbuf("pick_r", [P, BLOCKS, S], F32)
+        c_raw = {j0: sbuf("c_raw%d" % j0, [P, PACK, j1 - j0], F32) for j0, j1 in C_LOADS}
+        c_bf = [sbuf("c_bf%d" % j0, [P, j1 - j0, PACK], BF16) for j0, j1 in CHUNKS]
+        c_w = [sbuf("c_w%d" % j0, [P, j1 - j0], U32) for j0, j1 in CHUNKS]
+        c_s = [sbuf("c_s%d" % j0, [P, j1 - j0], U8) for j0, j1 in CHUNKS]
+        bank_blocks = {}
         banks = {}
-        staged = {}
-        for q in range(CHUNKS):
-            for h in range(BLOCKS // PAIR):
-                banks[q, h] = psum.tile([P, PAIR, CHUNK], F32, name="bank%d_%d" % (q, h))
-                staged[q, h] = keep.tile([P, PAIR, CHUNK], F32, name="staged%d_%d" % (q, h), align_bytes=64)
+        for q, (j0, j1) in enumerate(CHUNKS):
+            per_bank = BANK // (j1 - j0)
+            for h in range(BLOCKS // per_bank):
+                bank_blocks[q, h] = range(h * per_bank, (h + 1) * per_bank)
+                banks[q, h] = psum.tile([P, per_bank, j1 - j0], F32, name="bank%d_%d" % (q, h))
 
         c_rows = c.rearrange("(p t) j -> p t j", t=PACK)
         out_rows = out.rearrange("(b p) j -> p b j", p=P)
 
-        def load_scales(plane, rows):
+        def load_scales(queue, plane, rows):
             for r in range(4):
-                nc.sync.dma_start(out=plane[r:P:32, :].bitcast(I32), in_=rows[r:16:4, :].bitcast(I32))
-
-        def load_scales_by_quadrant(plane, rows):
-            for quad in range(4):
-                nc.sync.dma_start(
-                    out=plane[32 * quad : 32 * quad + 4, :].bitcast(I32), in_=rows[4 * quad : 4 * quad + 4, :].bitcast(I32)
-                )
+                queue.dma_start(out=plane[r:P:32, :].bitcast(I32), in_=rows[r:16:4, :].bitcast(I32))
 
         def load_res(b):
             nc.sync.dma_start(out=res[b][:], in_=rT[b * P : (b + 1) * P, :])
 
-        def load_c(q):
-            nc.sync.dma_start(out=c_raw[q][:], in_=c_rows[:, :, q * CHUNK : (q + 1) * CHUNK])
+        def load_c(i):
+            j0, j1 = C_LOADS[i]
+            nc.sync.dma_start(out=c_raw[j0][:], in_=c_rows[:, :, j0:j1])
 
-        def interleave(dst, raw):
-            nc.scalar.copy(
-                out=dst[:].rearrange("p (g i) t -> p g t i", i=4),
+        def load_offs():
+            nc.sync.dma_start(offsets[:], offs)
+
+        def load_tab():
+            nc.sync.dma_start(out=tab_w[:].bitcast(I32), in_=tab_words[0].rearrange("p t i -> p (t i)").bitcast(I32))
+
+        def load_w4():
+            nc.sync.dma_start(out=w4_w[:].bitcast(I32), in_=w4_words[0].bitcast(I32))
+            load_scales(nc.sync, w4_s, w4_scales[0])
+
+        def load_u():
+            nc.sync.dma_start(out=u_raw[:], in_=u.rearrange("(p t) n -> p t n", t=PACK))
+
+        def interleave(copy, dst, raw):
+            copy(
+                out=dst.rearrange("p (g i) t -> p g t i", i=4),
                 in_=raw.rearrange("p t (g i) -> p g t i", i=4),
             )
 
         def quantize(words, scales, grouped):
             nc.vector.quantize_mx(
-                out=words.bitcast(FP8X4), scales=scales, in_=grouped[:].rearrange("p w t -> p (w t)")
+                out=words[:].bitcast(FP8X4), scales=scales[:], in_=grouped[:].rearrange("p w t -> p (w t)")
             )
 
         def gather_res(b, j0, j1):
@@ -94,25 +105,25 @@ def tile_list_tabres_none_kernel(
             )
 
         def table_passes(q, h):
+            j0, j1 = CHUNKS[q]
+            step = BANK if j1 - j0 == BANK else N_FP4
             first = True
-            for e in range(PAIR):
-                b = PAIR * h + e
-                for j0 in range(0, CHUNK, N_FP4):
-                    cols = slice(q * CHUNK + j0, q * CHUNK + j0 + N_FP4)
+            for e, b in enumerate(bank_blocks[q, h]):
+                for j in range(j0, j1, step):
                     nc.tensor.matmul_mx(
-                        out=banks[q, h][:, e, j0 : j0 + N_FP4],
+                        out=banks[q, h][:, e, j - j0 : j - j0 + step],
                         lhsT=w4_w[:, 2 * b * P : 2 * (b + 1) * P].bitcast(FP4X4),
                         lhsT_scale=w4_s[:, b * P : (b + 1) * P],
-                        rhs=pick_w[:, cols].bitcast(FP8X4),
-                        rhs_scale=pick_s[:, cols],
+                        rhs=pick_w[:, j : j + step].bitcast(FP8X4),
+                        rhs_scale=pick_s[:, j : j + step],
                         start=first,
                         stop=False,
                     )
                     first = False
 
         def feature_passes(q, h):
-            for e in range(PAIR):
-                b = PAIR * h + e
+            blocks = bank_blocks[q, h]
+            for e, b in enumerate(blocks):
                 nc.tensor.matmul_mx(
                     out=banks[q, h][:, e, :],
                     lhsT=u_w[:, b * P : (b + 1) * P].bitcast(FP8X4),
@@ -120,62 +131,70 @@ def tile_list_tabres_none_kernel(
                     rhs=c_w[q][:].bitcast(FP8X4),
                     rhs_scale=c_s[q][:],
                     start=False,
-                    stop=(e == PAIR - 1),
+                    stop=(e == len(blocks) - 1),
                 )
 
-        def finish(q, h):
-            cols = slice(q * CHUNK, (q + 1) * CHUNK)
-            blocks = slice(PAIR * h, PAIR * (h + 1))
-            nc.vector.tensor_tensor(out=staged[q, h][:], in0=banks[q, h][:], in1=pick_r[:, blocks, cols], op=ADD)
-            nc.sync.dma_start(out=out_rows[:, blocks, cols], in_=staged[q, h][:])
+        def bank_part(q, b0, b1):
+            h = [key[1] for key in bank_blocks if key[0] == q and b0 in bank_blocks[key]][0]
+            first = bank_blocks[q, h].start
+            return banks[q, h][:, b0 - first : b1 - first, :]
 
-        def prepare_c(q):
-            interleave(c_bf[q], c_raw[q][:])
-            quantize(c_w[q][:], c_s[q][:], c_bf[q])
-            for h in range(BLOCKS // PAIR):
-                feature_passes(q, h)
+        def store(staged, b0, b1, j0, j1):
+            nc.sync.dma_start(out=out_rows[:, b0:b1, j0:j1], in_=staged[:])
+
+        def finish_on_vector(b0, b1, q):
+            j0, j1 = CHUNKS[q]
+            staged = sbuf("staged%d_%d" % (b0, q), [P, b1 - b0, j1 - j0], F32)
+            nc.vector.tensor_tensor(out=staged[:], in0=bank_part(q, b0, b1), in1=pick_r[:, b0:b1, j0:j1], op=ADD)
+            store(staged, b0, b1, j0, j1)
+
+        def finish_on_gpsimd(b0, b1, q0, q1):
+            j0, j1 = CHUNKS[q0][0], CHUNKS[q1 - 1][1]
+            staged = sbuf("staged%d_%d" % (b0, q0), [P, b1 - b0, j1 - j0], F32)
+            sums = sbuf("sums%d_%d" % (b0, q0), [P, b1 - b0, j1 - j0], F32)
+            for q in range(q0, q1):
+                nc.scalar.copy(out=sums[:, :, CHUNKS[q][0] - j0 : CHUNKS[q][1] - j0], in_=bank_part(q, b0, b1))
+            nc.gpsimd.tensor_tensor(out=staged[:], in0=sums[:], in1=pick_r[:, b0:b1, j0:j1], op=ADD)
+            store(staged, b0, b1, j0, j1)
+
+        def cast_c(copy, q, j0, j1):
+            interleave(copy, c_bf[q][:, j0:j1, :], c_raw[CHUNKS[q][0]][:, :, j0:j1])
+
+        def quantize_c(q):
+            quantize(c_w[q], c_s[q], c_bf[q])
+            for key in bank_blocks:
+                if key[0] == q:
+                    feature_passes(*key)
 
         nc.vector.memset(tab_s[:].bitcast(I32), 0)
-
-        nc.sync.dma_start(offsets[:], offs)
-        load_scales_by_quadrant(tab_rows, tab_scales[0])
-        nc.sync.dma_start(out=tab_w[:].bitcast(I32), in_=tab_words[0].rearrange("p t i -> p (t i)").bitcast(I32))
-        nc.sync.dma_start(out=u_raw[:], in_=u.rearrange("(p t) n -> p t n", t=PACK))
+        load_offs()
+        load_tab()
+        load_scales(nc.sync, tab_s, tab_scales[0])
         load_res(0)
-        nc.sync.dma_start(out=w4_w[:].bitcast(I32), in_=w4_words[0].bitcast(I32))
-        load_scales(w4_s, w4_scales[0])
-        load_res(1)
-        load_res(2)
+        load_u()
+        load_w4()
         load_c(0)
-        load_res(3)
-        for q in range(1, CHUNKS):
-            load_c(q)
-
-        for quad in range(0, P, 32):
-            live = slice(quad, quad + 4)
-            nc.vector.tensor_copy(out=tab_s[live, :].bitcast(I32), in_=tab_rows[live, :].bitcast(I32))
-        nc.vector.tensor_copy(out=pick_s[:], in_=tab_s[:].indirect(offsets[:]))
+        load_c(1)
+        for b in range(1, BLOCKS):
+            load_res(b)
         nc.vector.tensor_copy(out=pick_w[:], in_=tab_w[:].indirect(offsets[:]))
-        for h in range(M // CHUNK):
-            cols = slice(h * CHUNK, (h + 1) * CHUNK)
-            interleave(u_bf[h], u_raw[:, :, cols])
-            quantize(u_w[:, cols], u_s[:, cols], u_bf[h])
-        for q in range(CHUNKS):
-            for h in range(BLOCKS // PAIR):
-                table_passes(q, h)
+        nc.vector.tensor_copy(out=pick_s[:], in_=tab_s[:].indirect(offsets[:]))
+        interleave(nc.scalar.copy, u_bf[:], u_raw[:])
+        cast_c(nc.scalar.copy, 0, 0, 512)
+        for key in bank_blocks:
+            table_passes(*key)
+        gather_res(0, 0, S)
+        quantize(u_w, u_s, u_bf)
+        quantize_c(0)
+        cast_c(nc.vector.tensor_copy, 1, 0, 256)
+        cast_c(nc.scalar.copy, 1, 256, 512)
+        quantize_c(1)
         for b in range(BLOCKS - 1):
-            gather_res(b, 0, S)
-        last = BLOCKS - 1
-        prepare_c(0)
-        finish(0, 0)
-        gather_res(last, 0, CHUNK)
-        gather_res(last, CHUNK, 2 * CHUNK)
-        finish(0, 1)
-        gather_res(last, 2 * CHUNK, 3 * CHUNK)
-        prepare_c(1)
-        gather_res(last, 3 * CHUNK, S)
-        for q in range(1, CHUNKS):
-            if q + 1 < CHUNKS:
-                prepare_c(q + 1)
-            finish(q, 0)
-            finish(q, 1)
+            if b > 0:
+                gather_res(b, 0, S)
+            finish_on_gpsimd(b, b + 1, 0, 1)
+            finish_on_gpsimd(b, b + 1, 1, 2)
+        gather_res(3, 0, 512)
+        finish_on_vector(3, 4, 0)
+        gather_res(3, 512, S)
+        finish_on_vector(3, 4, 1)

@@ -22,7 +22,7 @@ BANK = 512
 N_FP4 = 128
 STRIPE = 16
 CHUNKS = ((0, 512), (512, 1024))
-C_LOADS = CHUNKS
+C_LOADS = ((0, 256), (256, 768), (768, 1024))
 
 
 def tile_list_tabres_none_kernel(
@@ -62,7 +62,6 @@ def tile_list_tabres_none_kernel(
                 banks[q, h] = psum.tile([P, per_bank, j1 - j0], F32, name="bank%d_%d" % (q, h))
 
         c_rows = c.rearrange("(p t) j -> p t j", t=PACK)
-        out_rows = out.rearrange("(b p) j -> p b j", p=P)
 
         def load_scales(queue, plane, rows):
             for r in range(4):
@@ -104,67 +103,49 @@ def tile_list_tabres_none_kernel(
                 out=pick_r[:, b, j0:j1], in_=res[b][:].indirect(offsets[:, j0 // STRIPE : j1 // STRIPE])
             )
 
-        def table_passes(q, h):
+        def table_pass(q, b, start):
             j0, j1 = CHUNKS[q]
-            step = BANK if j1 - j0 == BANK else N_FP4
-            first = True
-            for e, b in enumerate(bank_blocks[q, h]):
-                for j in range(j0, j1, step):
-                    nc.tensor.matmul_mx(
-                        out=banks[q, h][:, e, j - j0 : j - j0 + step],
-                        lhsT=w4_w[:, 2 * b * P : 2 * (b + 1) * P].bitcast(FP4X4),
-                        lhsT_scale=w4_s[:, b * P : (b + 1) * P],
-                        rhs=pick_w[:, j : j + step].bitcast(FP8X4),
-                        rhs_scale=pick_s[:, j : j + step],
-                        start=first,
-                        stop=False,
-                    )
-                    first = False
+            nc.tensor.matmul_mx(
+                out=banks[q, b][:, 0, :],
+                lhsT=w4_w[:, 2 * b * P : 2 * (b + 1) * P].bitcast(FP4X4),
+                lhsT_scale=w4_s[:, b * P : (b + 1) * P],
+                rhs=pick_w[:, j0:j1].bitcast(FP8X4),
+                rhs_scale=pick_s[:, j0:j1],
+                start=start,
+                stop=not start,
+            )
 
-        def feature_passes(q, h):
-            blocks = bank_blocks[q, h]
-            for e, b in enumerate(blocks):
-                nc.tensor.matmul_mx(
-                    out=banks[q, h][:, e, :],
-                    lhsT=u_w[:, b * P : (b + 1) * P].bitcast(FP8X4),
-                    lhsT_scale=u_s[:, b * P : (b + 1) * P],
-                    rhs=c_w[q][:].bitcast(FP8X4),
-                    rhs_scale=c_s[q][:],
-                    start=False,
-                    stop=(e == len(blocks) - 1),
-                )
+        def feature_pass(q, b, start):
+            nc.tensor.matmul_mx(
+                out=banks[q, b][:, 0, :],
+                lhsT=u_w[:, b * P : (b + 1) * P].bitcast(FP8X4),
+                lhsT_scale=u_s[:, b * P : (b + 1) * P],
+                rhs=c_w[q][:].bitcast(FP8X4),
+                rhs_scale=c_s[q][:],
+                start=start,
+                stop=not start,
+            )
 
-        def bank_part(q, b0, b1):
-            h = [key[1] for key in bank_blocks if key[0] == q and b0 in bank_blocks[key]][0]
-            first = bank_blocks[q, h].start
-            return banks[q, h][:, b0 - first : b1 - first, :]
+        staged = [sbuf("staged%d" % b, [P, S], F32) for b in range(BLOCKS)]
+        sums = [sbuf("sums%d" % b, [P, S], F32) for b in range(BLOCKS)]
 
-        def store(staged, b0, b1, j0, j1):
-            nc.sync.dma_start(out=out_rows[:, b0:b1, j0:j1], in_=staged[:])
+        def store(b):
+            nc.sync.dma_start(out=out[b * P : (b + 1) * P, :], in_=staged[b][:])
 
-        def finish_on_vector(b0, b1, q):
+        def add_on_vector(b, q):
             j0, j1 = CHUNKS[q]
-            staged = sbuf("staged%d_%d" % (b0, q), [P, b1 - b0, j1 - j0], F32)
-            nc.vector.tensor_tensor(out=staged[:], in0=bank_part(q, b0, b1), in1=pick_r[:, b0:b1, j0:j1], op=ADD)
-            store(staged, b0, b1, j0, j1)
+            nc.vector.tensor_tensor(out=staged[b][:, j0:j1], in0=banks[q, b][:, 0, :], in1=pick_r[:, b, j0:j1], op=ADD)
 
-        def finish_on_gpsimd(b0, b1, q0, q1):
+        def add_on_gpsimd(b, q0, q1):
             j0, j1 = CHUNKS[q0][0], CHUNKS[q1 - 1][1]
-            staged = sbuf("staged%d_%d" % (b0, q0), [P, b1 - b0, j1 - j0], F32)
-            sums = sbuf("sums%d_%d" % (b0, q0), [P, b1 - b0, j1 - j0], F32)
             for q in range(q0, q1):
-                nc.scalar.copy(out=sums[:, :, CHUNKS[q][0] - j0 : CHUNKS[q][1] - j0], in_=bank_part(q, b0, b1))
-            nc.gpsimd.tensor_tensor(out=staged[:], in0=sums[:], in1=pick_r[:, b0:b1, j0:j1], op=ADD)
-            store(staged, b0, b1, j0, j1)
+                nc.scalar.copy(out=sums[b][:, CHUNKS[q][0] : CHUNKS[q][1]], in_=banks[q, b][:, 0, :])
+            nc.gpsimd.tensor_tensor(out=staged[b][:, j0:j1], in0=sums[b][:, j0:j1], in1=pick_r[:, b, j0:j1], op=ADD)
 
-        def cast_c(copy, q, j0, j1):
-            interleave(copy, c_bf[q][:, j0:j1, :], c_raw[CHUNKS[q][0]][:, :, j0:j1])
-
-        def quantize_c(q):
-            quantize(c_w[q], c_s[q], c_bf[q])
-            for key in bank_blocks:
-                if key[0] == q:
-                    feature_passes(*key)
+        def cast_c(copy, j0, j1):
+            first = max(a for a, b in C_LOADS if a <= j0)
+            q = j0 // BANK
+            interleave(copy, c_bf[q][:, j0 - q * BANK : j1 - q * BANK, :], c_raw[first][:, :, j0 - first : j1 - first])
 
         nc.vector.memset(tab_s[:].bitcast(I32), 0)
         load_offs()
@@ -175,26 +156,39 @@ def tile_list_tabres_none_kernel(
         load_w4()
         load_c(0)
         load_c(1)
+        load_c(2)
         for b in range(1, BLOCKS):
             load_res(b)
         nc.vector.tensor_copy(out=pick_w[:], in_=tab_w[:].indirect(offsets[:]))
         nc.vector.tensor_copy(out=pick_s[:], in_=tab_s[:].indirect(offsets[:]))
         interleave(nc.scalar.copy, u_bf[:], u_raw[:])
-        cast_c(nc.scalar.copy, 0, 0, 512)
-        for key in bank_blocks:
-            table_passes(*key)
         gather_res(0, 0, S)
         quantize(u_w, u_s, u_bf)
-        quantize_c(0)
-        cast_c(nc.vector.tensor_copy, 1, 0, 256)
-        cast_c(nc.scalar.copy, 1, 256, 512)
-        quantize_c(1)
-        for b in range(BLOCKS - 1):
-            if b > 0:
-                gather_res(b, 0, S)
-            finish_on_gpsimd(b, b + 1, 0, 1)
-            finish_on_gpsimd(b, b + 1, 1, 2)
+        for q in range(2):
+            for b in range(BLOCKS):
+                table_pass(q, b, True)
+        cast_c(nc.scalar.copy, 0, 256)
+        cast_c(nc.scalar.copy, 512, 768)
+        cast_c(nc.vector.tensor_copy, 256, 512)
+        quantize(c_w[0], c_s[0], c_bf[0])
+        for b in range(BLOCKS):
+            feature_pass(0, b, False)
+        cast_c(nc.vector.tensor_copy, 768, 1024)
+        quantize(c_w[1], c_s[1], c_bf[1])
+        for b in range(BLOCKS):
+            feature_pass(1, b, False)
+        add_on_gpsimd(0, 0, 1)
+        add_on_gpsimd(0, 1, 2)
+        store(0)
+        gather_res(1, 0, S)
+        add_on_gpsimd(1, 0, 2)
+        store(1)
+        gather_res(2, 0, S)
+        add_on_gpsimd(2, 0, 1)
         gather_res(3, 0, 512)
-        finish_on_vector(3, 4, 0)
+        add_on_vector(2, 1)
+        store(2)
+        add_on_gpsimd(3, 0, 1)
         gather_res(3, 512, S)
-        finish_on_vector(3, 4, 1)
+        add_on_vector(3, 1)
+        store(3)

@@ -22,7 +22,7 @@ BANK = 512
 N_FP4 = 128
 STRIPE = 16
 CHUNKS = ((0, 512), (512, 1024))
-C_LOADS = ((0, 256), (256, 768), (768, 1024))
+C_LOADS = ((0, 768), (768, 1024))
 
 
 def tile_list_tabres_none_kernel(
@@ -129,12 +129,13 @@ def tile_list_tabres_none_kernel(
         staged = [sbuf("staged%d" % b, [P, S], F32) for b in range(BLOCKS)]
         sums = [sbuf("sums%d" % b, [P, S], F32) for b in range(BLOCKS)]
 
-        def store(b):
-            nc.sync.dma_start(out=out[b * P : (b + 1) * P, :], in_=staged[b][:])
+        def store(b, j0=0, j1=S):
+            nc.sync.dma_start(out=out[b * P : (b + 1) * P, j0:j1], in_=staged[b][:, j0:j1])
 
-        def add_on_vector(b, q):
-            j0, j1 = CHUNKS[q]
-            nc.vector.tensor_tensor(out=staged[b][:, j0:j1], in0=banks[q, b][:, 0, :], in1=pick_r[:, b, j0:j1], op=ADD)
+        def add_on_vector(b, j0, j1):
+            q = j0 // BANK
+            part = banks[q, b][:, 0, j0 - q * BANK : j1 - q * BANK]
+            nc.vector.tensor_tensor(out=staged[b][:, j0:j1], in0=part, in1=pick_r[:, b, j0:j1], op=ADD)
 
         def add_on_gpsimd(b, q0, q1):
             j0, j1 = CHUNKS[q0][0], CHUNKS[q1 - 1][1]
@@ -148,15 +149,14 @@ def tile_list_tabres_none_kernel(
             interleave(copy, c_bf[q][:, j0 - q * BANK : j1 - q * BANK, :], c_raw[first][:, :, j0 - first : j1 - first])
 
         nc.vector.memset(tab_s[:].bitcast(I32), 0)
-        load_offs()
         load_tab()
+        load_offs()
         load_scales(nc.sync, tab_s, tab_scales[0])
         load_res(0)
         load_u()
         load_w4()
         load_c(0)
         load_c(1)
-        load_c(2)
         for b in range(1, BLOCKS):
             load_res(b)
         nc.vector.tensor_copy(out=pick_w[:], in_=tab_w[:].indirect(offsets[:]))
@@ -185,10 +185,15 @@ def tile_list_tabres_none_kernel(
         store(1)
         gather_res(2, 0, S)
         add_on_gpsimd(2, 0, 1)
+        store(2, 0, 512)
         gather_res(3, 0, 512)
-        add_on_vector(2, 1)
-        store(2)
+        add_on_vector(2, 512, S)
+        store(2, 512, S)
         add_on_gpsimd(3, 0, 1)
-        gather_res(3, 512, S)
-        add_on_vector(3, 1)
-        store(3)
+        store(3, 0, 512)
+        gather_res(3, 512, 768)
+        gather_res(3, 768, S)
+        add_on_vector(3, 512, 768)
+        store(3, 512, 768)
+        add_on_vector(3, 768, S)
+        store(3, 768, S)

@@ -19,10 +19,9 @@ P = 128
 PACK = 4
 BLOCKS = M // P
 BANK = 512
-N_FP4 = 128
+HALVES = S // BANK
 STRIPE = 16
-CHUNKS = ((0, 512), (512, 1024))
-C_LOADS = ((0, 768), (768, 1024))
+C_SPLIT = 640
 
 
 def tile_list_tabres_none_kernel(
@@ -42,50 +41,26 @@ def tile_list_tabres_none_kernel(
         w4_w = sbuf("w4_w", [P, 2 * M], U8)
         w4_s = sbuf("w4_s", [P, M], U8)
         u_raw = sbuf("u_raw", [P, PACK, M], F32)
-        u_bf = sbuf("u_bf", [P, M, PACK], BF16)
-        u_w = sbuf("u_w", [P, M], U32)
-        u_s = sbuf("u_s", [P, M], U8)
+        u_bf = [sbuf("u_bf%d" % b, [P, P, PACK], BF16) for b in range(BLOCKS)]
+        u_w = [sbuf("u_w%d" % b, [P, P], U32) for b in range(BLOCKS)]
+        u_s = [sbuf("u_s%d" % b, [P, P], U8) for b in range(BLOCKS)]
         pick_w = sbuf("pick_w", [P, S], U32)
         pick_s = sbuf("pick_s", [P, S], U8)
         res = [sbuf("res%d" % b, [P, T], F32) for b in range(BLOCKS)]
-        pick_r = sbuf("pick_r", [P, BLOCKS, S], F32)
-        c_raw = {j0: sbuf("c_raw%d" % j0, [P, PACK, j1 - j0], F32) for j0, j1 in C_LOADS}
-        c_bf = [sbuf("c_bf%d" % j0, [P, j1 - j0, PACK], BF16) for j0, j1 in CHUNKS]
-        c_w = [sbuf("c_w%d" % j0, [P, j1 - j0], U32) for j0, j1 in CHUNKS]
-        c_s = [sbuf("c_s%d" % j0, [P, j1 - j0], U8) for j0, j1 in CHUNKS]
-        bank_blocks = {}
+        c_raw = sbuf("c_raw", [P, PACK, S], F32)
+        c_bf = [sbuf("c_bf%d" % q, [P, BANK, PACK], BF16) for q in range(HALVES)]
+        c_w = [sbuf("c_w%d" % q, [P, BANK], U32) for q in range(HALVES)]
+        c_s = [sbuf("c_s%d" % q, [P, BANK], U8) for q in range(HALVES)]
+        sums = [sbuf("sums%d" % b, [P, S], F32) for b in range(BLOCKS)]
+        staged = [sbuf("staged%d" % b, [P, S], F32) for b in range(BLOCKS)]
         banks = {}
-        for q, (j0, j1) in enumerate(CHUNKS):
-            per_bank = BANK // (j1 - j0)
-            for h in range(BLOCKS // per_bank):
-                bank_blocks[q, h] = range(h * per_bank, (h + 1) * per_bank)
-                banks[q, h] = psum.tile([P, per_bank, j1 - j0], F32, name="bank%d_%d" % (q, h))
-
-        c_rows = c.rearrange("(p t) j -> p t j", t=PACK)
+        for q in range(HALVES):
+            for b in range(BLOCKS):
+                banks[q, b] = psum.tile([P, BANK], F32, name="bank%d_%d" % (q, b))
 
         def load_scales(queue, plane, rows):
             for r in range(4):
                 queue.dma_start(out=plane[r:P:32, :].bitcast(I32), in_=rows[r:16:4, :].bitcast(I32))
-
-        def load_res(b):
-            nc.sync.dma_start(out=res[b][:], in_=rT[b * P : (b + 1) * P, :])
-
-        def load_c(i):
-            j0, j1 = C_LOADS[i]
-            nc.sync.dma_start(out=c_raw[j0][:], in_=c_rows[:, :, j0:j1])
-
-        def load_offs():
-            nc.sync.dma_start(offsets[:], offs)
-
-        def load_tab():
-            nc.sync.dma_start(out=tab_w[:].bitcast(I32), in_=tab_words[0].rearrange("p t i -> p (t i)").bitcast(I32))
-
-        def load_w4():
-            nc.sync.dma_start(out=w4_w[:].bitcast(I32), in_=w4_words[0].bitcast(I32))
-            load_scales(nc.sync, w4_s, w4_scales[0])
-
-        def load_u():
-            nc.sync.dma_start(out=u_raw[:], in_=u.rearrange("(p t) n -> p t n", t=PACK))
 
         def interleave(copy, dst, raw):
             copy(
@@ -98,102 +73,73 @@ def tile_list_tabres_none_kernel(
                 out=words[:].bitcast(FP8X4), scales=scales[:], in_=grouped[:].rearrange("p w t -> p (w t)")
             )
 
-        def gather_res(b, j0, j1):
-            nc.vector.tensor_copy(
-                out=pick_r[:, b, j0:j1], in_=res[b][:].indirect(offsets[:, j0 // STRIPE : j1 // STRIPE])
-            )
+        def cast_c(copy, j0, j1):
+            q = j0 // BANK
+            interleave(copy, c_bf[q][:, j0 - q * BANK : j1 - q * BANK, :], c_raw[:, :, j0:j1])
 
-        def table_pass(q, b, start):
-            j0, j1 = CHUNKS[q]
+        def cast_u(copy, b):
+            interleave(copy, u_bf[b][:], u_raw[:, :, b * P : (b + 1) * P])
+
+        def table_pass(q, b):
             nc.tensor.matmul_mx(
-                out=banks[q, b][:, 0, :],
+                out=banks[q, b][:],
                 lhsT=w4_w[:, 2 * b * P : 2 * (b + 1) * P].bitcast(FP4X4),
                 lhsT_scale=w4_s[:, b * P : (b + 1) * P],
-                rhs=pick_w[:, j0:j1].bitcast(FP8X4),
-                rhs_scale=pick_s[:, j0:j1],
-                start=start,
-                stop=not start,
+                rhs=pick_w[:, q * BANK : (q + 1) * BANK].bitcast(FP8X4),
+                rhs_scale=pick_s[:, q * BANK : (q + 1) * BANK],
+                start=True,
+                stop=False,
             )
 
-        def feature_pass(q, b, start):
+        def feature_pass(q, b):
             nc.tensor.matmul_mx(
-                out=banks[q, b][:, 0, :],
-                lhsT=u_w[:, b * P : (b + 1) * P].bitcast(FP8X4),
-                lhsT_scale=u_s[:, b * P : (b + 1) * P],
+                out=banks[q, b][:],
+                lhsT=u_w[b][:].bitcast(FP8X4),
+                lhsT_scale=u_s[b][:],
                 rhs=c_w[q][:].bitcast(FP8X4),
                 rhs_scale=c_s[q][:],
-                start=start,
-                stop=not start,
+                start=False,
+                stop=True,
             )
 
-        staged = [sbuf("staged%d" % b, [P, S], F32) for b in range(BLOCKS)]
-        sums = [sbuf("sums%d" % b, [P, S], F32) for b in range(BLOCKS)]
-
-        def store(b, j0=0, j1=S):
+        def finish(b, j0, j1):
+            nc.vector.tensor_tensor(
+                out=staged[b][:, j0:j1],
+                in0=res[b][:].indirect(offsets[:, j0 // STRIPE : j1 // STRIPE]),
+                in1=sums[b][:, j0:j1],
+                op=ADD,
+            )
             nc.sync.dma_start(out=out[b * P : (b + 1) * P, j0:j1], in_=staged[b][:, j0:j1])
 
-        def add_on_vector(b, j0, j1):
-            q = j0 // BANK
-            part = banks[q, b][:, 0, j0 - q * BANK : j1 - q * BANK]
-            nc.vector.tensor_tensor(out=staged[b][:, j0:j1], in0=part, in1=pick_r[:, b, j0:j1], op=ADD)
-
-        def add_on_gpsimd(b, q0, q1):
-            j0, j1 = CHUNKS[q0][0], CHUNKS[q1 - 1][1]
-            for q in range(q0, q1):
-                nc.scalar.copy(out=sums[b][:, CHUNKS[q][0] : CHUNKS[q][1]], in_=banks[q, b][:, 0, :])
-            nc.gpsimd.tensor_tensor(out=staged[b][:, j0:j1], in0=sums[b][:, j0:j1], in1=pick_r[:, b, j0:j1], op=ADD)
-
-        def cast_c(copy, j0, j1):
-            first = max(a for a, b in C_LOADS if a <= j0)
-            q = j0 // BANK
-            interleave(copy, c_bf[q][:, j0 - q * BANK : j1 - q * BANK, :], c_raw[first][:, :, j0 - first : j1 - first])
-
         nc.vector.memset(tab_s[:].bitcast(I32), 0)
-        load_tab()
-        load_offs()
+        nc.sync.dma_start(out=tab_w[:].bitcast(I32), in_=tab_words[0].rearrange("p t i -> p (t i)").bitcast(I32))
+        nc.sync.dma_start(offsets[:], offs)
         load_scales(nc.sync, tab_s, tab_scales[0])
-        load_res(0)
-        load_u()
-        load_w4()
-        load_c(0)
-        load_c(1)
-        for b in range(1, BLOCKS):
-            load_res(b)
+        nc.sync.dma_start(out=c_raw[:], in_=c.rearrange("(p t) j -> p t j", t=PACK))
+        nc.sync.dma_start(out=w4_w[:].bitcast(I32), in_=w4_words[0].bitcast(I32))
+        load_scales(nc.sync, w4_s, w4_scales[0])
+        nc.sync.dma_start(out=u_raw[:], in_=u.rearrange("(p t) n -> p t n", t=PACK))
+        for b in range(BLOCKS):
+            nc.sync.dma_start(out=res[b][:], in_=rT[b * P : (b + 1) * P, :])
+
         nc.vector.tensor_copy(out=pick_w[:], in_=tab_w[:].indirect(offsets[:]))
         nc.vector.tensor_copy(out=pick_s[:], in_=tab_s[:].indirect(offsets[:]))
-        interleave(nc.scalar.copy, u_bf[:], u_raw[:])
-        gather_res(0, 0, S)
-        quantize(u_w, u_s, u_bf)
-        for q in range(2):
-            for b in range(BLOCKS):
-                table_pass(q, b, True)
-        cast_c(nc.scalar.copy, 0, 256)
-        cast_c(nc.scalar.copy, 512, 768)
-        cast_c(nc.vector.tensor_copy, 256, 512)
-        quantize(c_w[0], c_s[0], c_bf[0])
+        cast_c(nc.scalar.copy, C_SPLIT, S)
+        cast_c(nc.vector.tensor_copy, 0, BANK)
+        cast_c(nc.vector.tensor_copy, BANK, C_SPLIT)
+        for q in range(HALVES):
+            quantize(c_w[q], c_s[q], c_bf[q])
         for b in range(BLOCKS):
-            feature_pass(0, b, False)
-        cast_c(nc.vector.tensor_copy, 768, 1024)
-        quantize(c_w[1], c_s[1], c_bf[1])
+            cast_u(nc.scalar.copy if b < 2 else nc.vector.tensor_copy, b)
         for b in range(BLOCKS):
-            feature_pass(1, b, False)
-        add_on_gpsimd(0, 0, 1)
-        add_on_gpsimd(0, 1, 2)
-        store(0)
-        gather_res(1, 0, S)
-        add_on_gpsimd(1, 0, 2)
-        store(1)
-        gather_res(2, 0, S)
-        add_on_gpsimd(2, 0, 1)
-        store(2, 0, 512)
-        gather_res(3, 0, 512)
-        add_on_vector(2, 512, S)
-        store(2, 512, S)
-        add_on_gpsimd(3, 0, 1)
-        store(3, 0, 512)
-        gather_res(3, 512, 768)
-        gather_res(3, 768, S)
-        add_on_vector(3, 512, 768)
-        store(3, 512, 768)
-        add_on_vector(3, 768, S)
-        store(3, 768, S)
+            quantize(u_w[b], u_s[b], u_bf[b])
+            for q in range(HALVES):
+                table_pass(q, b)
+            for q in range(HALVES):
+                feature_pass(q, b)
+                nc.scalar.copy(out=sums[b][:, q * BANK : (q + 1) * BANK], in_=banks[q, b][:])
+        for b in range(BLOCKS - 1):
+            finish(b, 0, S)
+        finish(BLOCKS - 1, 0, 512)
+        finish(BLOCKS - 1, 512, 768)
+        finish(BLOCKS - 1, 768, S)

@@ -21,7 +21,8 @@ BLOCKS = M // P
 BANK = 512
 HALVES = S // BANK
 STRIPE = 16
-C_SPLIT = 640
+C_SPLIT = 352
+ZERO_SPLIT = 352
 
 
 def tile_list_tabres_none_kernel(
@@ -40,14 +41,15 @@ def tile_list_tabres_none_kernel(
         tab_s = sbuf("tab_s", [P, T], U8)
         w4_w = sbuf("w4_w", [P, 2 * M], U8)
         w4_s = sbuf("w4_s", [P, M], U8)
-        u_raw = sbuf("u_raw", [P, PACK, M], F32)
-        u_bf = [sbuf("u_bf%d" % b, [P, P, PACK], BF16) for b in range(BLOCKS)]
-        u_w = [sbuf("u_w%d" % b, [P, P], U32) for b in range(BLOCKS)]
-        u_s = [sbuf("u_s%d" % b, [P, P], U8) for b in range(BLOCKS)]
-        pick_w = sbuf("pick_w", [P, S], U32)
-        pick_s = sbuf("pick_s", [P, S], U8)
+        u_raw = [sbuf("u_raw%d" % h, [P, PACK, 2 * P], F32) for h in range(2)]
+        u_parts = ((0, 1), (1, 2), (2, 4))
+        u_bf = {b0: sbuf("u_bf%d" % b0, [P, (b1 - b0) * P, PACK], BF16) for b0, b1 in u_parts}
+        u_w = {b0: sbuf("u_w%d" % b0, [P, (b1 - b0) * P], U32) for b0, b1 in u_parts}
+        u_s = {b0: sbuf("u_s%d" % b0, [P, (b1 - b0) * P], U8) for b0, b1 in u_parts}
+        pick_w = [sbuf("pick_w%d" % q, [P, BANK], U32) for q in range(HALVES)]
+        pick_s = [sbuf("pick_s%d" % q, [P, BANK], U8) for q in range(HALVES)]
         res = [sbuf("res%d" % b, [P, T], F32) for b in range(BLOCKS)]
-        c_raw = sbuf("c_raw", [P, PACK, S], F32)
+        c_raw = [sbuf("c_raw%d" % q, [P, PACK, BANK], F32) for q in range(HALVES)]
         c_bf = [sbuf("c_bf%d" % q, [P, BANK, PACK], BF16) for q in range(HALVES)]
         c_w = [sbuf("c_w%d" % q, [P, BANK], U32) for q in range(HALVES)]
         c_s = [sbuf("c_s%d" % q, [P, BANK], U8) for q in range(HALVES)]
@@ -73,29 +75,30 @@ def tile_list_tabres_none_kernel(
                 out=words[:].bitcast(FP8X4), scales=scales[:], in_=grouped[:].rearrange("p w t -> p (w t)")
             )
 
-        def cast_c(copy, j0, j1):
-            q = j0 // BANK
-            interleave(copy, c_bf[q][:, j0 - q * BANK : j1 - q * BANK, :], c_raw[:, :, j0:j1])
+        def cast_c(copy, q, j0, j1):
+            interleave(copy, c_bf[q][:, j0:j1, :], c_raw[q][:, :, j0:j1])
 
-        def cast_u(copy, b):
-            interleave(copy, u_bf[b][:], u_raw[:, :, b * P : (b + 1) * P])
+        def entries(j0, j1):
+            return offsets[:, j0 // STRIPE : j1 // STRIPE]
 
         def table_pass(q, b):
             nc.tensor.matmul_mx(
                 out=banks[q, b][:],
                 lhsT=w4_w[:, 2 * b * P : 2 * (b + 1) * P].bitcast(FP4X4),
                 lhsT_scale=w4_s[:, b * P : (b + 1) * P],
-                rhs=pick_w[:, q * BANK : (q + 1) * BANK].bitcast(FP8X4),
-                rhs_scale=pick_s[:, q * BANK : (q + 1) * BANK],
+                rhs=pick_w[q][:].bitcast(FP8X4),
+                rhs_scale=pick_s[q][:],
                 start=True,
                 stop=False,
             )
 
         def feature_pass(q, b):
+            b0 = min(b, 2)
+            cols = slice((b - b0) * P, (b - b0 + 1) * P)
             nc.tensor.matmul_mx(
                 out=banks[q, b][:],
-                lhsT=u_w[b][:].bitcast(FP8X4),
-                lhsT_scale=u_s[b][:],
+                lhsT=u_w[b0][:, cols].bitcast(FP8X4),
+                lhsT_scale=u_s[b0][:, cols],
                 rhs=c_w[q][:].bitcast(FP8X4),
                 rhs_scale=c_s[q][:],
                 start=False,
@@ -105,40 +108,67 @@ def tile_list_tabres_none_kernel(
         def finish(b, j0, j1):
             nc.vector.tensor_tensor(
                 out=staged[b][:, j0:j1],
-                in0=res[b][:].indirect(offsets[:, j0 // STRIPE : j1 // STRIPE]),
+                in0=res[b][:].indirect(entries(j0, j1)),
                 in1=sums[b][:, j0:j1],
                 op=ADD,
             )
             nc.sync.dma_start(out=out[b * P : (b + 1) * P, j0:j1], in_=staged[b][:, j0:j1])
 
-        nc.vector.memset(tab_s[:].bitcast(I32), 0)
-        nc.sync.dma_start(out=tab_w[:].bitcast(I32), in_=tab_words[0].rearrange("p t i -> p (t i)").bitcast(I32))
-        nc.sync.dma_start(offsets[:], offs)
-        load_scales(nc.sync, tab_s, tab_scales[0])
-        nc.sync.dma_start(out=c_raw[:], in_=c.rearrange("(p t) j -> p t j", t=PACK))
-        nc.sync.dma_start(out=w4_w[:].bitcast(I32), in_=w4_words[0].bitcast(I32))
-        load_scales(nc.sync, w4_s, w4_scales[0])
-        nc.sync.dma_start(out=u_raw[:], in_=u.rearrange("(p t) n -> p t n", t=PACK))
-        for b in range(BLOCKS):
+        def load_res(b):
             nc.sync.dma_start(out=res[b][:], in_=rT[b * P : (b + 1) * P, :])
 
-        nc.vector.tensor_copy(out=pick_w[:], in_=tab_w[:].indirect(offsets[:]))
-        nc.vector.tensor_copy(out=pick_s[:], in_=tab_s[:].indirect(offsets[:]))
-        cast_c(nc.scalar.copy, C_SPLIT, S)
-        cast_c(nc.vector.tensor_copy, 0, BANK)
-        cast_c(nc.vector.tensor_copy, BANK, C_SPLIT)
-        for q in range(HALVES):
-            quantize(c_w[q], c_s[q], c_bf[q])
-        for b in range(BLOCKS):
-            cast_u(nc.scalar.copy if b < 2 else nc.vector.tensor_copy, b)
-        for b in range(BLOCKS):
-            quantize(u_w[b], u_s[b], u_bf[b])
-            for q in range(HALVES):
-                table_pass(q, b)
+        def load_c(q):
+            nc.sync.dma_start(out=c_raw[q][:], in_=c_rows[:, :, q * BANK : (q + 1) * BANK])
+
+        def load_u(h):
+            nc.sync.dma_start(out=u_raw[h][:], in_=u_rows[:, :, 2 * h * P : 2 * (h + 1) * P])
+
+        def prepare_u(b0, b1):
+            h = b0 // 2
+            interleave(nc.scalar.copy, u_bf[b0][:], u_raw[h][:, :, (b0 - 2 * h) * P : (b1 - 2 * h) * P])
+            quantize(u_w[b0], u_s[b0], u_bf[b0])
+
+        def sum_block(b):
             for q in range(HALVES):
                 feature_pass(q, b)
                 nc.scalar.copy(out=sums[b][:, q * BANK : (q + 1) * BANK], in_=banks[q, b][:])
-        for b in range(BLOCKS - 1):
+
+        c_rows = c.rearrange("(p t) j -> p t j", t=PACK)
+        u_rows = u.rearrange("(p t) n -> p t n", t=PACK)
+        nc.vector.memset(tab_s[:].bitcast(I32)[:, :ZERO_SPLIT], 0)
+        nc.gpsimd.memset(tab_s[:].bitcast(I32)[:, ZERO_SPLIT:], 0)
+        nc.sync.dma_start(out=tab_w[:].bitcast(I32), in_=tab_words[0].rearrange("p t i -> p (t i)").bitcast(I32))
+        nc.sync.dma_start(offsets[:], offs)
+        load_scales(nc.sync, tab_s, tab_scales[0])
+        nc.sync.dma_start(out=w4_w[:].bitcast(I32), in_=w4_words[0].bitcast(I32))
+        load_c(0)
+        load_scales(nc.sync, w4_s, w4_scales[0])
+        load_c(1)
+        load_u(0)
+        load_res(0)
+        load_u(1)
+        for b in range(1, BLOCKS):
+            load_res(b)
+
+        for q in range(HALVES):
+            nc.vector.tensor_copy(out=pick_w[q][:], in_=tab_w[:].indirect(entries(q * BANK, (q + 1) * BANK)))
+            nc.vector.tensor_copy(out=pick_s[q][:], in_=tab_s[:].indirect(entries(q * BANK, (q + 1) * BANK)))
+            for b in range(BLOCKS):
+                table_pass(q, b)
+        cast_c(nc.scalar.copy, 0, 0, BANK)
+        cast_c(nc.scalar.copy, 1, C_SPLIT, BANK)
+        cast_c(nc.vector.tensor_copy, 1, 0, C_SPLIT)
+        for q in range(HALVES):
+            quantize(c_w[q], c_s[q], c_bf[q])
+        prepare_u(0, 1)
+        prepare_u(1, 2)
+        sum_block(0)
+        finish(0, 0, 512)
+        finish(0, 512, S)
+        prepare_u(2, 4)
+        for b in range(1, BLOCKS):
+            sum_block(b)
+        for b in range(1, BLOCKS - 1):
             finish(b, 0, S)
         finish(BLOCKS - 1, 0, 512)
         finish(BLOCKS - 1, 512, 768)

@@ -21,8 +21,6 @@ BLOCKS = M // P
 BANK = 512
 HALVES = S // BANK
 STRIPE = 16
-C_SPLIT = 352
-ZERO_SPLIT = 352
 
 
 def tile_list_tabres_none_kernel(
@@ -41,15 +39,15 @@ def tile_list_tabres_none_kernel(
         tab_s = sbuf("tab_s", [P, T], U8)
         w4_w = sbuf("w4_w", [P, 2 * M], U8)
         w4_s = sbuf("w4_s", [P, M], U8)
-        u_raw = [sbuf("u_raw%d" % h, [P, PACK, 2 * P], F32) for h in range(2)]
+        u_raw = sbuf("u_raw", [P, PACK, M], F32)
         u_parts = ((0, 1), (1, 2), (2, 4))
         u_bf = {b0: sbuf("u_bf%d" % b0, [P, (b1 - b0) * P, PACK], BF16) for b0, b1 in u_parts}
         u_w = {b0: sbuf("u_w%d" % b0, [P, (b1 - b0) * P], U32) for b0, b1 in u_parts}
         u_s = {b0: sbuf("u_s%d" % b0, [P, (b1 - b0) * P], U8) for b0, b1 in u_parts}
-        pick_w = [sbuf("pick_w%d" % q, [P, BANK], U32) for q in range(HALVES)]
+        pick_w = sbuf("pick_w", [P, S], U32)
         pick_s = [sbuf("pick_s%d" % q, [P, BANK], U8) for q in range(HALVES)]
         res = [sbuf("res%d" % b, [P, T], F32) for b in range(BLOCKS)]
-        c_raw = [sbuf("c_raw%d" % q, [P, PACK, BANK], F32) for q in range(HALVES)]
+        c_raw = sbuf("c_raw", [P, PACK, S], F32)
         c_bf = [sbuf("c_bf%d" % q, [P, BANK, PACK], BF16) for q in range(HALVES)]
         c_w = [sbuf("c_w%d" % q, [P, BANK], U32) for q in range(HALVES)]
         c_s = [sbuf("c_s%d" % q, [P, BANK], U8) for q in range(HALVES)]
@@ -75,8 +73,9 @@ def tile_list_tabres_none_kernel(
                 out=words[:].bitcast(FP8X4), scales=scales[:], in_=grouped[:].rearrange("p w t -> p (w t)")
             )
 
-        def cast_c(copy, q, j0, j1):
-            interleave(copy, c_bf[q][:, j0:j1, :], c_raw[q][:, :, j0:j1])
+        def cast_c(copy, j0, j1):
+            q = j0 // BANK
+            interleave(copy, c_bf[q][:, j0 - q * BANK : j1 - q * BANK, :], c_raw[:, :, j0:j1])
 
         def entries(j0, j1):
             return offsets[:, j0 // STRIPE : j1 // STRIPE]
@@ -86,7 +85,7 @@ def tile_list_tabres_none_kernel(
                 out=banks[q, b][:],
                 lhsT=w4_w[:, 2 * b * P : 2 * (b + 1) * P].bitcast(FP4X4),
                 lhsT_scale=w4_s[:, b * P : (b + 1) * P],
-                rhs=pick_w[q][:].bitcast(FP8X4),
+                rhs=pick_w[:, q * BANK : (q + 1) * BANK].bitcast(FP8X4),
                 rhs_scale=pick_s[q][:],
                 start=True,
                 stop=False,
@@ -105,27 +104,22 @@ def tile_list_tabres_none_kernel(
                 stop=True,
             )
 
-        def finish(b, j0, j1):
+        def add_residual(b, j0, j1):
             nc.vector.tensor_tensor(
                 out=staged[b][:, j0:j1],
                 in0=res[b][:].indirect(entries(j0, j1)),
                 in1=sums[b][:, j0:j1],
                 op=ADD,
             )
+
+        def store(b, j0, j1):
             nc.sync.dma_start(out=out[b * P : (b + 1) * P, j0:j1], in_=staged[b][:, j0:j1])
 
-        def load_res(b):
-            nc.sync.dma_start(out=res[b][:], in_=rT[b * P : (b + 1) * P, :])
+        def load_c(t0, t1):
+            nc.sync.dma_start(out=c_raw[:, t0:t1, :], in_=c_rows[:, t0:t1, :])
 
-        def load_c(q):
-            nc.sync.dma_start(out=c_raw[q][:], in_=c_rows[:, :, q * BANK : (q + 1) * BANK])
-
-        def load_u(h):
-            nc.sync.dma_start(out=u_raw[h][:], in_=u_rows[:, :, 2 * h * P : 2 * (h + 1) * P])
-
-        def prepare_u(b0, b1):
-            h = b0 // 2
-            interleave(nc.scalar.copy, u_bf[b0][:], u_raw[h][:, :, (b0 - 2 * h) * P : (b1 - 2 * h) * P])
+        def prepare_u(copy, b0, b1):
+            interleave(copy, u_bf[b0][:], u_raw[:, :, b0 * P : b1 * P])
             quantize(u_w[b0], u_s[b0], u_bf[b0])
 
         def sum_block(b):
@@ -134,42 +128,39 @@ def tile_list_tabres_none_kernel(
                 nc.scalar.copy(out=sums[b][:, q * BANK : (q + 1) * BANK], in_=banks[q, b][:])
 
         c_rows = c.rearrange("(p t) j -> p t j", t=PACK)
-        u_rows = u.rearrange("(p t) n -> p t n", t=PACK)
-        nc.vector.memset(tab_s[:].bitcast(I32)[:, :ZERO_SPLIT], 0)
-        nc.gpsimd.memset(tab_s[:].bitcast(I32)[:, ZERO_SPLIT:], 0)
+        nc.vector.memset(tab_s[:].bitcast(I32), 0)
         nc.sync.dma_start(out=tab_w[:].bitcast(I32), in_=tab_words[0].rearrange("p t i -> p (t i)").bitcast(I32))
         nc.sync.dma_start(offsets[:], offs)
         load_scales(nc.sync, tab_s, tab_scales[0])
         nc.sync.dma_start(out=w4_w[:].bitcast(I32), in_=w4_words[0].bitcast(I32))
-        load_c(0)
+        load_c(0, 2)
         load_scales(nc.sync, w4_s, w4_scales[0])
-        load_c(1)
-        load_u(0)
-        load_res(0)
-        load_u(1)
-        for b in range(1, BLOCKS):
-            load_res(b)
+        load_c(2, 4)
+        nc.sync.dma_start(out=u_raw[:], in_=u.rearrange("(p t) n -> p t n", t=PACK))
+        for b in range(BLOCKS):
+            nc.sync.dma_start(out=res[b][:], in_=rT[b * P : (b + 1) * P, :])
 
+        nc.vector.tensor_copy(out=pick_w[:], in_=tab_w[:].indirect(offsets[:]))
         for q in range(HALVES):
-            nc.vector.tensor_copy(out=pick_w[q][:], in_=tab_w[:].indirect(entries(q * BANK, (q + 1) * BANK)))
             nc.vector.tensor_copy(out=pick_s[q][:], in_=tab_s[:].indirect(entries(q * BANK, (q + 1) * BANK)))
             for b in range(BLOCKS):
                 table_pass(q, b)
-        cast_c(nc.scalar.copy, 0, 0, BANK)
-        cast_c(nc.scalar.copy, 1, C_SPLIT, BANK)
-        cast_c(nc.vector.tensor_copy, 1, 0, C_SPLIT)
-        for q in range(HALVES):
-            quantize(c_w[q], c_s[q], c_bf[q])
-        prepare_u(0, 1)
-        prepare_u(1, 2)
+        cast_c(nc.scalar.copy, BANK, S)
+        cast_c(nc.vector.tensor_copy, 0, BANK)
+        quantize(c_w[0], c_s[0], c_bf[0])
+        prepare_u(nc.vector.tensor_copy, 0, 1)
+        quantize(c_w[1], c_s[1], c_bf[1])
+        prepare_u(nc.scalar.copy, 1, 2)
         sum_block(0)
-        finish(0, 0, 512)
-        finish(0, 512, S)
-        prepare_u(2, 4)
+        prepare_u(nc.scalar.copy, 2, 4)
         for b in range(1, BLOCKS):
             sum_block(b)
+        add_residual(0, 0, BANK)
+        add_residual(0, BANK, S)
+        store(0, 0, S)
         for b in range(1, BLOCKS - 1):
-            finish(b, 0, S)
-        finish(BLOCKS - 1, 0, 512)
-        finish(BLOCKS - 1, 512, 768)
-        finish(BLOCKS - 1, 768, S)
+            add_residual(b, 0, S)
+            store(b, 0, S)
+        for j0, j1 in ((0, 512), (512, 768), (768, S)):
+            add_residual(BLOCKS - 1, j0, j1)
+            store(BLOCKS - 1, j0, j1)

@@ -118,8 +118,10 @@ def tile_list_tabres_none_kernel(
         def load_c(t0, t1):
             nc.sync.dma_start(out=c_raw[:, t0:t1, :], in_=c_rows[:, t0:t1, :])
 
-        def prepare_u(copy, b0, b1):
+        def cast_u(copy, b0, b1):
             interleave(copy, u_bf[b0][:], u_raw[:, :, b0 * P : b1 * P])
+
+        def quantize_u(b0):
             quantize(u_w[b0], u_s[b0], u_bf[b0])
 
         def sum_block(b):
@@ -148,12 +150,14 @@ def tile_list_tabres_none_kernel(
         cast_c(nc.scalar.copy, BANK, S)
         cast_c(nc.vector.tensor_copy, 0, BANK)
         quantize(c_w[0], c_s[0], c_bf[0])
-        prepare_u(nc.vector.tensor_copy, 0, 1)
+        cast_u(nc.vector.tensor_copy, 0, 1)
+        quantize_u(0)
         quantize(c_w[1], c_s[1], c_bf[1])
-        prepare_u(nc.scalar.copy, 1, 2)
-        sum_block(0)
-        prepare_u(nc.scalar.copy, 2, 4)
-        for b in range(1, BLOCKS):
+        cast_u(nc.vector.tensor_copy, 1, 2)
+        cast_u(nc.scalar.copy, 2, 4)
+        quantize_u(2)
+        quantize_u(1)
+        for b in range(BLOCKS):
             sum_block(b)
         add_residual(0, 0, BANK)
         add_residual(0, BANK, S)

@@ -165,6 +165,6 @@ def tile_list_tabres_none_kernel(
         for b in range(1, BLOCKS - 1):
             add_residual(b, 0, S)
             store(b, 0, S)
-        for j0, j1 in ((0, 512), (512, 768), (768, S)):
+        for j0, j1 in ((0, 512), (512, 864), (864, S)):
             add_residual(BLOCKS - 1, j0, j1)
             store(BLOCKS - 1, j0, j1)

@@ -53,6 +53,7 @@ def tile_list_tabres_none_kernel(
         c_s = [sbuf("c_s%d" % q, [P, BANK], U8) for q in range(HALVES)]
         sums = [sbuf("sums%d" % b, [P, S], F32) for b in range(BLOCKS)]
         staged = [sbuf("staged%d" % b, [P, S], F32) for b in range(BLOCKS)]
+        warm = sbuf("warm", [P, 16], F32)
         banks = {}
         for q in range(HALVES):
             for b in range(BLOCKS):
@@ -131,6 +132,8 @@ def tile_list_tabres_none_kernel(
 
         c_rows = c.rearrange("(p t) j -> p t j", t=PACK)
         nc.vector.memset(tab_s[:].bitcast(I32), 0)
+        nc.vector.memset(warm[:, 0:8], 0.0)
+        nc.scalar.copy(out=warm[:, 8:16], in_=warm[:, 0:8])
         nc.sync.dma_start(out=tab_w[:].bitcast(I32), in_=tab_words[0].rearrange("p t i -> p (t i)").bitcast(I32))
         nc.sync.dma_start(offsets[:], offs)
         load_scales(nc.sync, tab_s, tab_scales[0])

@@ -29,35 +29,37 @@ def tile_list_tabres_none_kernel(
     nc = tc.nc
     with ExitStack() as ctx:
         keep = ctx.enter_context(tc.tile_pool(name="keep", bufs=1))
+        shared = ctx.enter_context(tc.tile_pool(name="shared", bufs=1))
         psum = ctx.enter_context(tc.psum_pool(name="psum", bufs=1))
 
-        def sbuf(name, shape, dtype):
-            return keep.tile(shape, dtype, name=name, align_bytes=64)
+        def sbuf(name, shape, dtype, tag=None):
+            return keep.tile(shape, dtype, name=name, tag=tag or name, align_bytes=64)
 
         offsets = keep.tile([P, S // STRIPE], U16, name="offsets")
         tab_w = sbuf("tab_w", [P, T], U32)
         tab_s = sbuf("tab_s", [P, T], U8)
-        w4_w = sbuf("w4_w", [P, 2 * M], U8)
+        w4_parts = ((0, 2), (2, 4))
+        w4_w = [sbuf("w4_w%d" % b0, [P, 2 * (b1 - b0) * P], U8) for b0, b1 in w4_parts]
         w4_s = sbuf("w4_s", [P, M], U8)
         u_raw = sbuf("u_raw", [P, PACK, M], F32)
         u_parts = ((0, 1), (1, 2), (2, 4))
-        u_bf = {b0: sbuf("u_bf%d" % b0, [P, (b1 - b0) * P, PACK], BF16) for b0, b1 in u_parts}
+        u_bf = {b0: sbuf("u_bf%d" % b0, [P, (b1 - b0) * P, PACK], BF16) for b0, b1 in u_parts[1:]}
+        u_bf[0] = shared.tile([P, P, PACK], BF16, name="u_bf0", offset=512, align_bytes=64)
         u_w = {b0: sbuf("u_w%d" % b0, [P, (b1 - b0) * P], U32) for b0, b1 in u_parts}
         u_s = {b0: sbuf("u_s%d" % b0, [P, (b1 - b0) * P], U8) for b0, b1 in u_parts}
         pick_w = sbuf("pick_w", [P, S], U32)
-        pick_s = [sbuf("pick_s%d" % q, [P, BANK], U8) for q in range(HALVES)]
+        pick_s = sbuf("pick_s", [P, S], U8)
         res = [sbuf("res%d" % b, [P, T], F32) for b in range(BLOCKS)]
         c_raw = sbuf("c_raw", [P, PACK, S], F32)
-        c_bf = [sbuf("c_bf%d" % q, [P, BANK, PACK], BF16) for q in range(HALVES)]
-        c_w = [sbuf("c_w%d" % q, [P, BANK], U32) for q in range(HALVES)]
-        c_s = [sbuf("c_s%d" % q, [P, BANK], U8) for q in range(HALVES)]
+        c_cuts = (0, BANK, 768, S)
+        c_bf = [sbuf("c_bf%d" % i, [P, c_cuts[i + 1] - c_cuts[i], PACK], BF16) for i in range(3)]
+        c_w = [sbuf("c_w%d" % i, [P, c_cuts[i + 1] - c_cuts[i]], U32) for i in range(3)]
+        c_s = [sbuf("c_s%d" % i, [P, c_cuts[i + 1] - c_cuts[i]], U8) for i in range(2)]
+        c_s.append(shared.tile([P, S - c_cuts[2]], U8, name="c_s2", offset=1024, align_bytes=64))
         sums = [sbuf("sums%d" % b, [P, S], F32) for b in range(BLOCKS)]
         staged = [sbuf("staged%d" % b, [P, S], F32) for b in range(BLOCKS)]
         warm = sbuf("warm", [P, 16], F32)
         banks = {}
-        for q in range(HALVES):
-            for b in range(BLOCKS):
-                banks[q, b] = psum.tile([P, BANK], F32, name="bank%d_%d" % (q, b))
 
         def load_scales(queue, plane, rows):
             for r in range(4):
@@ -71,39 +73,45 @@ def tile_list_tabres_none_kernel(
 
         def quantize(words, scales, grouped):
             nc.vector.quantize_mx(
-                out=words[:].bitcast(FP8X4), scales=scales[:], in_=grouped[:].rearrange("p w t -> p (w t)")
+                out=words.bitcast(FP8X4), scales=scales, in_=grouped.rearrange("p w t -> p (w t)")
             )
 
         def cast_c(copy, j0, j1):
-            q = j0 // BANK
-            interleave(copy, c_bf[q][:, j0 - q * BANK : j1 - q * BANK, :], c_raw[:, :, j0:j1])
+            interleave(copy, c_bf[c_cuts.index(j0)][:], c_raw[:, :, j0:j1])
 
         def entries(j0, j1):
             return offsets[:, j0 // STRIPE : j1 // STRIPE]
 
-        def table_pass(q, b):
-            nc.tensor.matmul_mx(
-                out=banks[q, b][:],
-                lhsT=w4_w[:, 2 * b * P : 2 * (b + 1) * P].bitcast(FP4X4),
-                lhsT_scale=w4_s[:, b * P : (b + 1) * P],
-                rhs=pick_w[:, q * BANK : (q + 1) * BANK].bitcast(FP8X4),
-                rhs_scale=pick_s[q][:],
-                start=True,
-                stop=False,
-            )
+        def table_passes(b, j0, j1):
+            banks[b, j0] = psum.tile([P, j1 - j0], F32, name="bank%d_%d" % (b, j0), tag="bank%d" % (len(banks) % 8))
+            width = BANK if j1 - j0 == BANK else P
+            for j in range(j0, j1, width):
+                nc.tensor.matmul_mx(
+                    out=banks[b, j0][:, j - j0 : j - j0 + width],
+                    lhsT=w4_w[b // 2][:, 2 * (b % 2) * P : 2 * (b % 2 + 1) * P].bitcast(FP4X4),
+                    lhsT_scale=w4_s[:, b * P : (b + 1) * P],
+                    rhs=pick_w[:, j : j + width].bitcast(FP8X4),
+                    rhs_scale=pick_s[:, j : j + width],
+                    start=j == j0,
+                    stop=False,
+                )
 
-        def feature_pass(q, b):
+        def feature_passes(b, j0, j1):
             b0 = min(b, 2)
-            cols = slice((b - b0) * P, (b - b0 + 1) * P)
-            nc.tensor.matmul_mx(
-                out=banks[q, b][:],
-                lhsT=u_w[b0][:, cols].bitcast(FP8X4),
-                lhsT_scale=u_s[b0][:, cols],
-                rhs=c_w[q][:].bitcast(FP8X4),
-                rhs_scale=c_s[q][:],
-                start=False,
-                stop=True,
-            )
+            rows = slice((b - b0) * P, (b - b0 + 1) * P)
+            cuts = [j0] + [j for j in c_cuts if j0 < j < j1] + [j1]
+            for ja, jb in zip(cuts, cuts[1:]):
+                i = max(n for n in range(3) if c_cuts[n] <= ja)
+                cols = slice(ja - c_cuts[i], jb - c_cuts[i])
+                nc.tensor.matmul_mx(
+                    out=banks[b, j0][:, ja - j0 : jb - j0],
+                    lhsT=u_w[b0][:, rows].bitcast(FP8X4),
+                    lhsT_scale=u_s[b0][:, rows],
+                    rhs=c_w[i][:, cols].bitcast(FP8X4),
+                    rhs_scale=c_s[i][:, cols],
+                    start=False,
+                    stop=jb == j1,
+                )
 
         def add_residual(b, j0, j1):
             nc.vector.tensor_tensor(
@@ -116,6 +124,10 @@ def tile_list_tabres_none_kernel(
         def store(b, j0, j1):
             nc.sync.dma_start(out=out[b * P : (b + 1) * P, j0:j1], in_=staged[b][:, j0:j1])
 
+        def load_w4(h):
+            b0, b1 = w4_parts[h]
+            nc.sync.dma_start(out=w4_w[h][:].bitcast(I32), in_=w4_words[0][:, 2 * b0 * P : 2 * b1 * P].bitcast(I32))
+
         def load_c(t0, t1):
             nc.sync.dma_start(out=c_raw[:, t0:t1, :], in_=c_rows[:, t0:t1, :])
 
@@ -123,12 +135,15 @@ def tile_list_tabres_none_kernel(
             interleave(copy, u_bf[b0][:], u_raw[:, :, b0 * P : b1 * P])
 
         def quantize_u(b0):
-            quantize(u_w[b0], u_s[b0], u_bf[b0])
+            quantize(u_w[b0][:], u_s[b0][:], u_bf[b0][:])
 
         def sum_block(b):
-            for q in range(HALVES):
-                feature_pass(q, b)
-                nc.scalar.copy(out=sums[b][:, q * BANK : (q + 1) * BANK], in_=banks[q, b][:])
+            cuts = (0, BANK // 2, BANK, S) if b == 0 else (0, BANK, S)
+            for j0, j1 in zip(cuts, cuts[1:]):
+                table_passes(b, j0, j1)
+            for j0, j1 in zip(cuts, cuts[1:]):
+                feature_passes(b, j0, j1)
+                nc.scalar.copy(out=sums[b][:, j0:j1], in_=banks[b, j0][:])
 
         c_rows = c.rearrange("(p t) j -> p t j", t=PACK)
         nc.vector.memset(tab_s[:].bitcast(I32), 0)
@@ -137,32 +152,32 @@ def tile_list_tabres_none_kernel(
         nc.sync.dma_start(out=tab_w[:].bitcast(I32), in_=tab_words[0].rearrange("p t i -> p (t i)").bitcast(I32))
         nc.sync.dma_start(offsets[:], offs)
         load_scales(nc.sync, tab_s, tab_scales[0])
-        nc.sync.dma_start(out=w4_w[:].bitcast(I32), in_=w4_words[0].bitcast(I32))
-        load_c(0, 2)
+        load_c(0, 4)
+        load_w4(0)
         load_scales(nc.sync, w4_s, w4_scales[0])
-        load_c(2, 4)
         nc.sync.dma_start(out=u_raw[:], in_=u.rearrange("(p t) n -> p t n", t=PACK))
         for b in range(BLOCKS):
             nc.sync.dma_start(out=res[b][:], in_=rT[b * P : (b + 1) * P, :])
+            if b == 0:
+                load_w4(1)
 
         nc.vector.tensor_copy(out=pick_w[:], in_=tab_w[:].indirect(offsets[:]))
-        for q in range(HALVES):
-            nc.vector.tensor_copy(out=pick_s[q][:], in_=tab_s[:].indirect(entries(q * BANK, (q + 1) * BANK)))
-            for b in range(BLOCKS):
-                table_pass(q, b)
-        cast_c(nc.scalar.copy, BANK, S)
+        nc.vector.tensor_copy(out=pick_s[:], in_=tab_s[:].indirect(offsets[:]))
+        cast_c(nc.scalar.copy, BANK, 768)
+        cast_c(nc.scalar.copy, 768, S)
         cast_c(nc.vector.tensor_copy, 0, BANK)
-        quantize(c_w[0], c_s[0], c_bf[0])
+        quantize(c_w[0][:], c_s[0][:], c_bf[0][:])
+        quantize(c_w[1][:], c_s[1][:], c_bf[1][:])
         cast_u(nc.vector.tensor_copy, 0, 1)
         quantize_u(0)
-        quantize(c_w[1], c_s[1], c_bf[1])
-        cast_u(nc.vector.tensor_copy, 1, 2)
-        cast_u(nc.scalar.copy, 2, 4)
-        quantize_u(2)
-        quantize_u(1)
+        quantize(c_w[2][:], c_s[2][:], c_bf[2][:])
+        for b0, b1 in u_parts[1:]:
+            cast_u(nc.scalar.copy, b0, b1)
+            quantize_u(b0)
         for b in range(BLOCKS):
             sum_block(b)
-        add_residual(0, 0, BANK)
+        add_residual(0, 0, BANK // 2)
+        add_residual(0, BANK // 2, BANK)
         add_residual(0, BANK, S)
         store(0, 0, S)
         for b in range(1, BLOCKS - 1):

@@ -58,7 +58,6 @@ def tile_list_tabres_none_kernel(
         c_s.append(shared.tile([P, S - c_cuts[2]], U8, name="c_s2", offset=1024, align_bytes=64))
         sums = [sbuf("sums%d" % b, [P, S], F32) for b in range(BLOCKS)]
         staged = [sbuf("staged%d" % b, [P, S], F32) for b in range(BLOCKS)]
-        warm = sbuf("warm", [P, 16], F32)
         banks = {}
 
         def load_scales(queue, plane, rows):
@@ -147,8 +146,6 @@ def tile_list_tabres_none_kernel(
 
         c_rows = c.rearrange("(p t) j -> p t j", t=PACK)
         nc.vector.memset(tab_s[:].bitcast(I32), 0)
-        nc.vector.memset(warm[:, 0:8], 0.0)
-        nc.scalar.copy(out=warm[:, 8:16], in_=warm[:, 0:8])
         nc.sync.dma_start(out=tab_w[:].bitcast(I32), in_=tab_words[0].rearrange("p t i -> p (t i)").bitcast(I32))
         nc.sync.dma_start(offsets[:], offs)
         load_scales(nc.sync, tab_s, tab_scales[0])

@@ -180,6 +180,6 @@ def tile_list_tabres_none_kernel(
         for b in range(1, BLOCKS - 1):
             add_residual(b, 0, S)
             store(b, 0, S)
-        for j0, j1 in ((0, 512), (512, 864), (864, S)):
+        for j0, j1 in ((0, 512), (512, 832), (832, S)):
             add_residual(BLOCKS - 1, j0, j1)
             store(BLOCKS - 1, j0, j1)

@@ -98,7 +98,7 @@ def tile_list_tabres_none_kernel(
         def feature_passes(b, j0, j1):
             b0 = min(b, 2)
             rows = slice((b - b0) * P, (b - b0 + 1) * P)
-            cuts = [j0] + [j for j in c_cuts if j0 < j < j1] + [j1]
+            cuts = [j0] + [j for j in (256,) + c_cuts if j0 < j < j1 and (j != 256 or j0 == P)] + [j1]
             for ja, jb in zip(cuts, cuts[1:]):
                 i = max(n for n in range(3) if c_cuts[n] <= ja)
                 cols = slice(ja - c_cuts[i], jb - c_cuts[i])
@@ -137,7 +137,7 @@ def tile_list_tabres_none_kernel(
             quantize(u_w[b0][:], u_s[b0][:], u_bf[b0][:])
 
         def sum_block(b):
-            cuts = (0, BANK // 2, BANK, S) if b == 0 else (0, BANK, S)
+            cuts = (0, P, BANK, S) if b == 0 else (0, BANK, S)
             for j0, j1 in zip(cuts, cuts[1:]):
                 table_passes(b, j0, j1)
             for j0, j1 in zip(cuts, cuts[1:]):
@@ -173,8 +173,8 @@ def tile_list_tabres_none_kernel(
             quantize_u(b0)
         for b in range(BLOCKS):
             sum_block(b)
-        add_residual(0, 0, BANK // 2)
-        add_residual(0, BANK // 2, BANK)
+        add_residual(0, 0, P)
+        add_residual(0, P, BANK)
         add_residual(0, BANK, S)
         store(0, 0, S)
         for b in range(1, BLOCKS - 1):

@@ -64,6 +64,12 @@ def tile_list_tabres_none_kernel(
             for r in range(4):
                 queue.dma_start(out=plane[r:P:32, :].bitcast(I32), in_=rows[r:16:4, :].bitcast(I32))
 
+        def load_scales_by_quadrant(queue, plane, rows):
+            for q in range(4):
+                queue.dma_start(
+                    out=plane[32 * q : 32 * q + 4, :].bitcast(I32), in_=rows[4 * q : 4 * q + 4, :].bitcast(I32)
+                )
+
         def interleave(copy, dst, raw):
             copy(
                 out=dst.rearrange("p (g i) t -> p g t i", i=4),
@@ -148,7 +154,7 @@ def tile_list_tabres_none_kernel(
         nc.vector.memset(tab_s[:].bitcast(I32), 0)
         nc.sync.dma_start(out=tab_w[:].bitcast(I32), in_=tab_words[0].rearrange("p t i -> p (t i)").bitcast(I32))
         nc.sync.dma_start(offsets[:], offs)
-        load_scales(nc.sync, tab_s, tab_scales[0])
+        load_scales_by_quadrant(nc.sync, tab_s, tab_scales[0])
         load_c(0, 4)
         load_w4(0)
         load_scales(nc.sync, w4_s, w4_scales[0])

from contextlib import ExitStack

import concourse.mybir as mybir

K, M, T, S = 512, 512, 2048, 1024
FLOPS = 2 * 2 * K * M * S

F32 = mybir.dt.float32
BF16 = mybir.dt.bfloat16
I32 = mybir.dt.int32
U32 = mybir.dt.uint32
U16 = mybir.dt.uint16
U8 = mybir.dt.uint8
FP8X4 = mybir.dt.float8_e4m3fn_x4
FP4X4 = mybir.dt.float4_e2m1fn_x4
ADD = mybir.AluOpType.add

P = 128
PACK = 4
BLOCKS = M // P
BANK = 512
HALVES = S // BANK
STRIPE = 16


def tile_list_tabres_none_kernel(
    tc, tab_words, tab_scales, w4_words, w4_scales, c, u, rT, offs, out
):
    nc = tc.nc
    with ExitStack() as ctx:
        keep = ctx.enter_context(tc.tile_pool(name="keep", bufs=1))
        shared = ctx.enter_context(tc.tile_pool(name="shared", bufs=1))
        psum = ctx.enter_context(tc.psum_pool(name="psum", bufs=1))

        def sbuf(name, shape, dtype, tag=None):
            return keep.tile(shape, dtype, name=name, tag=tag or name, align_bytes=64)

        offsets = keep.tile([P, S // STRIPE], U16, name="offsets")
        tab_w = sbuf("tab_w", [P, T], U32)
        tab_s = sbuf("tab_s", [P, T], U8)
        w4_parts = ((0, 2), (2, 4))
        w4_w = [sbuf("w4_w%d" % b0, [P, 2 * (b1 - b0) * P], U8) for b0, b1 in w4_parts]
        w4_s = sbuf("w4_s", [P, M], U8)
        u_raw = sbuf("u_raw", [P, PACK, M], F32)
        u_parts = ((0, 1), (1, 2), (2, 4))
        u_bf = {b0: sbuf("u_bf%d" % b0, [P, (b1 - b0) * P, PACK], BF16) for b0, b1 in u_parts[1:]}
        u_bf[0] = shared.tile([P, P, PACK], BF16, name="u_bf0", offset=512, align_bytes=64)
        u_w = {b0: sbuf("u_w%d" % b0, [P, (b1 - b0) * P], U32) for b0, b1 in u_parts}
        u_s = {b0: sbuf("u_s%d" % b0, [P, (b1 - b0) * P], U8) for b0, b1 in u_parts}
        pick_w = sbuf("pick_w", [P, S], U32)
        pick_s = sbuf("pick_s", [P, S], U8)
        res = [sbuf("res%d" % b, [P, T], F32) for b in range(BLOCKS)]
        c_raw = sbuf("c_raw", [P, PACK, S], F32)
        c_cuts = (0, BANK, 768, S)
        c_bf = [sbuf("c_bf%d" % i, [P, c_cuts[i + 1] - c_cuts[i], PACK], BF16) for i in range(3)]
        c_w = [sbuf("c_w%d" % i, [P, c_cuts[i + 1] - c_cuts[i]], U32) for i in range(3)]
        c_s = [sbuf("c_s%d" % i, [P, c_cuts[i + 1] - c_cuts[i]], U8) for i in range(2)]
        c_s.append(shared.tile([P, S - c_cuts[2]], U8, name="c_s2", offset=1024, align_bytes=64))
        sums = [sbuf("sums%d" % b, [P, S], F32) for b in range(BLOCKS)]
        staged = [sbuf("staged%d" % b, [P, S], F32) for b in range(BLOCKS)]
        banks = {}

        def load_scales(queue, plane, rows):
            for r in range(4):
                queue.dma_start(out=plane[r:P:32, :].bitcast(I32), in_=rows[r:16:4, :].bitcast(I32))

        def load_scales_by_quadrant(queue, plane, rows):
            for q in range(4):
                queue.dma_start(
                    out=plane[32 * q : 32 * q + 4, :].bitcast(I32), in_=rows[4 * q : 4 * q + 4, :].bitcast(I32)
                )

        def interleave(copy, dst, raw):
            copy(
                out=dst.rearrange("p (g i) t -> p g t i", i=4),
                in_=raw.rearrange("p t (g i) -> p g t i", i=4),
            )

        def quantize(words, scales, grouped):
            nc.vector.quantize_mx(
                out=words.bitcast(FP8X4), scales=scales, in_=grouped.rearrange("p w t -> p (w t)")
            )

        def cast_c(copy, j0, j1):
            interleave(copy, c_bf[c_cuts.index(j0)][:], c_raw[:, :, j0:j1])

        def entries(j0, j1):
            return offsets[:, j0 // STRIPE : j1 // STRIPE]

        def table_passes(b, j0, j1):
            banks[b, j0] = psum.tile([P, j1 - j0], F32, name="bank%d_%d" % (b, j0), tag="bank%d" % (len(banks) % 8))
            width = BANK if j1 - j0 == BANK else P
            for j in range(j0, j1, width):
                nc.tensor.matmul_mx(
                    out=banks[b, j0][:, j - j0 : j - j0 + width],
                    lhsT=w4_w[b // 2][:, 2 * (b % 2) * P : 2 * (b % 2 + 1) * P].bitcast(FP4X4),
                    lhsT_scale=w4_s[:, b * P : (b + 1) * P],
                    rhs=pick_w[:, j : j + width].bitcast(FP8X4),
                    rhs_scale=pick_s[:, j : j + width],
                    start=j == j0,
                    stop=False,
                )

        def feature_passes(b, j0, j1):
            b0 = min(b, 2)
            rows = slice((b - b0) * P, (b - b0 + 1) * P)
            cuts = [j0] + [j for j in (256,) + c_cuts if j0 < j < j1 and (j != 256 or j0 == P)] + [j1]
            for ja, jb in zip(cuts, cuts[1:]):
                i = max(n for n in range(3) if c_cuts[n] <= ja)
                cols = slice(ja - c_cuts[i], jb - c_cuts[i])
                nc.tensor.matmul_mx(
                    out=banks[b, j0][:, ja - j0 : jb - j0],
                    lhsT=u_w[b0][:, rows].bitcast(FP8X4),
                    lhsT_scale=u_s[b0][:, rows],
                    rhs=c_w[i][:, cols].bitcast(FP8X4),
                    rhs_scale=c_s[i][:, cols],
                    start=False,
                    stop=jb == j1,
                )

        def add_residual(b, j0, j1):
            nc.vector.tensor_tensor(
                out=staged[b][:, j0:j1],
                in0=res[b][:].indirect(entries(j0, j1)),
                in1=sums[b][:, j0:j1],
                op=ADD,
            )

        def store(b, j0, j1):
            nc.sync.dma_start(out=out[b * P : (b + 1) * P, j0:j1], in_=staged[b][:, j0:j1])

        def load_w4(h):
            b0, b1 = w4_parts[h]
            nc.sync.dma_start(out=w4_w[h][:].bitcast(I32), in_=w4_words[0][:, 2 * b0 * P : 2 * b1 * P].bitcast(I32))

        def load_c(t0, t1):
            nc.sync.dma_start(out=c_raw[:, t0:t1, :], in_=c_rows[:, t0:t1, :])

        def cast_u(copy, b0, b1):
            interleave(copy, u_bf[b0][:], u_raw[:, :, b0 * P : b1 * P])

        def quantize_u(b0):
            quantize(u_w[b0][:], u_s[b0][:], u_bf[b0][:])

        def sum_block(b):
            cuts = (0, P, BANK, S) if b == 0 else (0, BANK, S)
            for j0, j1 in zip(cuts, cuts[1:]):
                table_passes(b, j0, j1)
            for j0, j1 in zip(cuts, cuts[1:]):
                feature_passes(b, j0, j1)
                nc.scalar.copy(out=sums[b][:, j0:j1], in_=banks[b, j0][:])

        c_rows = c.rearrange("(p t) j -> p t j", t=PACK)
        nc.vector.memset(tab_s[:].bitcast(I32), 0)
        nc.sync.dma_start(out=tab_w[:].bitcast(I32), in_=tab_words[0].rearrange("p t i -> p (t i)").bitcast(I32))
        nc.sync.dma_start(offsets[:], offs)
        load_scales_by_quadrant(nc.sync, tab_s, tab_scales[0])
        load_c(0, 4)
        load_w4(0)
        load_scales(nc.sync, w4_s, w4_scales[0])
        nc.sync.dma_start(out=u_raw[:], in_=u.rearrange("(p t) n -> p t n", t=PACK))
        for b in range(BLOCKS):
            nc.sync.dma_start(out=res[b][:], in_=rT[b * P : (b + 1) * P, :])
            if b == 0:
                load_w4(1)

        nc.vector.tensor_copy(out=pick_w[:], in_=tab_w[:].indirect(offsets[:]))
        nc.vector.tensor_copy(out=pick_s[:], in_=tab_s[:].indirect(offsets[:]))
        cast_c(nc.scalar.copy, BANK, 768)
        cast_c(nc.scalar.copy, 768, S)
        cast_c(nc.vector.tensor_copy, 0, BANK)
        quantize(c_w[0][:], c_s[0][:], c_bf[0][:])
        quantize(c_w[1][:], c_s[1][:], c_bf[1][:])
        cast_u(nc.vector.tensor_copy, 0, 1)
        quantize_u(0)
        quantize(c_w[2][:], c_s[2][:], c_bf[2][:])
        for b0, b1 in u_parts[1:]:
            cast_u(nc.scalar.copy, b0, b1)
            quantize_u(b0)
        for b in range(BLOCKS):
            sum_block(b)
        add_residual(0, 0, P)
        add_residual(0, P, BANK)
        add_residual(0, BANK, S)
        store(0, 0, S)
        for b in range(1, BLOCKS - 1):
            add_residual(b, 0, S)
            store(b, 0, S)
        for j0, j1 in ((0, 512), (512, 832), (832, S)):
            add_residual(BLOCKS - 1, j0, j1)
            store(BLOCKS - 1, j0, j1)
